import numpy as np
import ml_dtypes


def mxq(x, axis, fmt="e4m3"):
    dtype, down = {"e4m3": (ml_dtypes.float8_e4m3fn, 7), "e5m2": (ml_dtypes.float8_e5m2, 14)}[fmt]
    v = np.moveaxis(np.asarray(x, np.float32).astype(ml_dtypes.bfloat16).astype(np.float64), axis, -1)
    blocks = v.reshape(v.shape[:-1] + (-1, 32))
    amax = np.abs(blocks).max(-1, keepdims=True)
    byte = np.maximum(np.where(amax > 0, np.frexp(amax)[1] - 1 + 127, 0) - down, 1)
    scale = np.exp2(byte - 127.0)
    codes = (blocks / scale).astype(np.float32).astype(dtype).astype(np.float64)
    return np.moveaxis((codes * scale).reshape(v.shape), -1, axis)


WIDE = False


def mx_kscale(k):
    if not WIDE:
        return np.ones(k)
    levels = np.array([10, -10, 5, -5, 0])
    if k % 512:
        return np.exp2(np.random.permutation(np.resize(levels, k // 32))).repeat(32)
    a = np.empty((k // 512, 16))
    for p in range(k // 512):
        a[p, :8] = np.random.permutation(np.resize(levels, 8))
        for g in range(8):
            far = levels[np.abs(levels - a[p, g]) >= 10]
            a[p, g + 8] = far[np.random.randint(len(far))]
    return np.exp2(a.ravel()).repeat(32)


def f64(x):
    return np.asarray(x).astype(np.float64)


def striped(idx):
    return np.tile(idx.reshape(-1, 16).T, (8, 1)).astype(np.uint16)


def unstriped(offs):
    return offs[:16].T.reshape(-1).astype(np.int64)


E2M1 = np.array([0.0, 0.5, 1.0, 1.5, 2.0, 3.0, 4.0, 6.0, -0.0, -0.5, -1.0, -1.5, -2.0, -3.0, -4.0, -6.0])


def pack_weight(w, fmt):
    k, n = w.shape
    w = f64(np.asarray(w, np.float32).astype(ml_dtypes.bfloat16)).reshape(k // 32, 32, n)
    amax = np.abs(w).max(1)
    if fmt == "e4m3":
        byte = np.frexp(amax)[1] - 1 + 127 - 7
    else:
        mant, ex = np.frexp(amax / 6.0)
        byte = np.where(mant > 0.5, ex, ex - 1) + 127
    byte = np.clip(np.where(amax > 0, byte, 1), 1, 254)
    scaled = (w * np.exp2(127.0 - byte)[:, None, :]).reshape(k, n).astype(np.float32)
    by_word = np.ascontiguousarray(scaled.reshape(k // 512, 128, 4, n).transpose(0, 1, 3, 2))
    if fmt == "e4m3":
        words = by_word.astype(ml_dtypes.float8_e4m3fn).view(np.uint8)
    else:
        c = by_word.astype(ml_dtypes.float4_e2m1fn).view(np.uint8) & 0xF
        words = (c[..., 0::2] | (c[..., 1::2] << 4)).reshape(k // 512, 128, 2 * n)
    return np.ascontiguousarray(words), np.ascontiguousarray(byte.astype(np.uint8).reshape(k // 512, 16, n))


def unpack_weight(words, scales, fmt):
    g, _, n = scales.shape
    words = np.ascontiguousarray(words).reshape(g, 128, n, -1)
    if fmt == "e4m3":
        vals = words.view(ml_dtypes.float8_e4m3fn).astype(np.float64)
    else:
        nib = np.empty((g, 128, n, 4), np.uint8)
        nib[..., 0::2] = words & 0xF
        nib[..., 1::2] = words >> 4
        vals = E2M1[nib]
    vals = vals * np.repeat(np.exp2(scales.astype(np.float64) - 127.0), 8, axis=1)[..., None]
    return vals.transpose(0, 1, 3, 2).reshape(g * 512, n)


def gelu(v):
    return 0.5 * v * (1.0 + np.tanh(np.sqrt(2.0 / np.pi) * (v + 0.044715 * v**3)))


K, H, N, T, S, P = 1024, 1024, 512, 4096, 1024, 512

def setup_inputs():
    n = np.random.standard_normal
    s = mx_kscale(K)[:, None]
    u = mx_kscale(H)[:, None]
    tab_words, tab_scales = pack_weight(n((K, T)) * s, "e4m3")
    w1 = (n((K, H)) / np.sqrt(K) / s * u.T).astype(np.float32)
    w2_words, w2_scales = pack_weight(n((H, N)) / np.sqrt(H) / u, "e2m1")
    b2 = (0.5 * n(N)).astype(np.float32)
    return {"tab_words": tab_words, "tab_scales": tab_scales,
            "offs": striped(np.random.permutation(T)[:S]),
            "pos1": striped(np.random.permutation(S)[:P]),
            "pos2": striped(np.random.permutation(S)[:P]),
            "w1": w1, "w2_words": w2_words, "w2_scales": w2_scales, "b2": b2}

def reference(tab_words, tab_scales, offs, pos1, pos2, w1, w2_words, w2_scales, b2):
    v = unpack_weight(tab_words, tab_scales, "e4m3")[:, unstriped(offs)]
    w1q = mxq(f64(w1), 0, "e4m3")
    w2 = unpack_weight(w2_words, w2_scales, "e2m1")
    h = np.square(w1q.T @ v)
    a = h[:, unstriped(pos1)]
    b = h[:, unstriped(pos2)]
    z = np.sqrt(a + b)
    zq = mxq(z, 0, "e4m3")
    y = (w2.T @ zq) + f64(b2)[:, None]
    return 1.0 / (1.0 + np.exp(-y))

@@ -1,0 +1,247 @@
+from contextlib import ExitStack
+
+import concourse.mybir as mybir
+from concourse.masks import make_identity
+
+K, H, N, T, S, PAIRS = 1024, 1024, 512, 4096, 1024, 512
+FLOPS = 2 * K * H * S + 2 * H * N * PAIRS
+
+F32 = mybir.dt.float32
+BF16 = mybir.dt.bfloat16
+I32 = mybir.dt.int32
+U32 = mybir.dt.uint32
+U16 = mybir.dt.uint16
+U8 = mybir.dt.uint8
+FP8X4 = mybir.dt.float8_e4m3fn_x4
+FP4X4 = mybir.dt.float4_e2m1fn_x4
+ACT = mybir.ActivationFunctionType
+
+P = 128
+PASSES = 2
+BANK = 512
+TILES = H // P
+CHUNKS = ((0, 1), (1, 1), (2, 1), (3, 1), (4, 2), (6, 2))
+
+
+def tile_list_seismic_arrival_score_kernel(tc, tab_words, tab_scales, offs, pos1, pos2, w1, w2_words, w2_scales, b2, out):
+    nc = tc.nc
+    with ExitStack() as ctx:
+        keep = ctx.enter_context(tc.tile_pool(name="keep", bufs=1))
+        ring = ctx.enter_context(tc.tile_pool(name="ring", bufs=4))
+        acc_pool = ctx.enter_context(tc.psum_pool(name="acc", bufs=4))
+        sum_pool = ctx.enter_context(tc.psum_pool(name="sums", bufs=2))
+        turn_pool = ctx.enter_context(tc.psum_pool(name="turn", bufs=2))
+
+        offs_sb = keep.tile([P, S // 16], U16, name="offs_sb")
+        pos1_sb = keep.tile([P, PAIRS // 16], U16, name="pos1_sb")
+        pos2_sb = keep.tile([P, PAIRS // 16], U16, name="pos2_sb")
+        tab_sb = [keep.tile([P, T], I32, name="tab%d" % a, align_bytes=64) for a in range(PASSES)]
+        tab_sc = keep.tile([P, T // 4], I32, name="tab_sc", align_bytes=64)
+        w2_sb = keep.tile([P, PASSES, 2 * N], U8, name="w2_sb", align_bytes=64)
+        w2_sc = keep.tile([P, PASSES, N // 4], I32, name="w2_sc", align_bytes=64)
+        bias = keep.tile([P, N // P], F32, name="bias")
+        warm = keep.tile([P, 2], F32, name="warm")
+        warm2 = keep.tile([P, 1], F32, name="warm2")
+        ident = keep.tile([P, P], F32, name="ident", align_bytes=64)
+        perm = keep.tile([P, P], F32, name="perm", align_bytes=64)
+
+        nc.vector.memset(tab_sc[:], 0)
+        nc.vector.memset(w2_sc[:], 0)
+        nc.vector.memset(warm[:, 0:1], 1.0)
+        nc.scalar.activation(warm[:, 1:2], warm[:, 0:1], ACT.Sqrt)
+
+        raw = {}
+
+        def load_w1(first, count, a):
+            t = keep.tile([P, 4, count * P], F32, name="raw%d_%d" % (first, a), align_bytes=64)
+            rows = w1[a * 512 : (a + 1) * 512, first * P : (first + count) * P]
+            nc.sync.dma_start(t[:], rows.rearrange("(p j) w -> p j w", j=4))
+            for c in range(count):
+                raw[(first + c, a)] = t[:, :, c * P : (c + 1) * P]
+
+        def load_tab(a):
+            nc.sync.dma_start(tab_sb[a][:], tab_words[a].rearrange("p t i -> p (t i)").bitcast(I32))
+
+        load_tab(0)
+        nc.sync.dma_start(offs_sb[:], offs)
+        for a in range(PASSES):
+            for q in range(4):
+                row = 32 * q + 4 * a
+                nc.sync.dma_start(tab_sc[row : row + 4, :], tab_scales[a, 4 * q : 4 * q + 4, :].bitcast(I32))
+        load_w1(0, 1, 0)
+        load_tab(1)
+        load_w1(0, 1, 1)
+        nc.sync.dma_start(pos1_sb[:], pos1)
+        nc.sync.dma_start(pos2_sb[:], pos2)
+        for first, count in CHUNKS[1:]:
+            for a in range(PASSES):
+                load_w1(first, count, a)
+        nc.sync.dma_start(w2_sb[:], w2_words.rearrange("a p n -> p a n"))
+        for q in range(4):
+            nc.sync.dma_start(
+                w2_sc[32 * q : 32 * q + 4, :, :],
+                w2_scales[:, 4 * q : 4 * q + 4, :].bitcast(I32).rearrange("a r n -> r a n"),
+            )
+        with nc.allow_non_contiguous_dma(reason="one bias value a partition"):
+            nc.sync.dma_start(bias[:], b2.rearrange("(t p) -> p t", p=P))
+
+        make_identity(nc, ident[:])
+        nc.vector.tensor_copy(
+            perm[:].rearrange("k (u p e) -> k u p e", u=2, e=2),
+            ident[:].rearrange("k (p u e) -> k u p e", u=2, e=2),
+        )
+
+        v_codes = [[keep.tile([P, BANK], U32, name="v%d_%d" % (a, b), align_bytes=64) for b in range(2)] for a in range(PASSES)]
+        v_sc = keep.tile([P, S], U8, name="v_sc", align_bytes=64)
+
+        def gather_tab(a, b):
+            nc.vector.tensor_copy(v_codes[a][b][:], tab_sb[a][:].bitcast(U32).indirect(offs_sb[:, 32 * b : 32 * (b + 1)]))
+
+        w_bf = [keep.tile([P, PASSES, P, 4], BF16, name="wbf%d" % c, align_bytes=64) for c in range(TILES)]
+        w_codes = [keep.tile([P, PASSES, P], U32, name="wc%d" % c, align_bytes=64) for c in range(TILES)]
+        w_sc = [keep.tile([P, PASSES, P], U8, name="ws%d" % c, align_bytes=64) for c in range(TILES)]
+
+        def cast(c, a):
+            nc.scalar.copy(
+                w_bf[c][:, a, :, :].rearrange("p (g i) t -> p g t i", i=4),
+                raw[(c, a)].rearrange("p t (g i) -> p g t i", i=4),
+            )
+
+        def quant_w(c, a0, a1):
+            nc.vector.quantize_mx(
+                out=w_codes[c][:, a0:a1, :].rearrange("p a m -> p (a m)").bitcast(FP8X4),
+                scales=w_sc[c][:, a0:a1, :].rearrange("p a m -> p (a m)"),
+                in_=w_bf[c][:, a0:a1, :, :].rearrange("p a m t -> p (a m t)"),
+            )
+
+        def mm1(c, bank, a, b):
+            nc.tensor.matmul_mx(
+                out=bank[:],
+                lhsT=w_codes[c][:, a, :].bitcast(FP8X4),
+                lhsT_scale=w_sc[c][:, a, :],
+                rhs=v_codes[a][b][:].bitcast(FP8X4),
+                rhs_scale=v_sc[4 * a : P, BANK * b : BANK * (b + 1)],
+                start=(a == 0),
+                stop=(a == PASSES - 1),
+            )
+
+        h = {}
+
+        def energy(c, order):
+            banks = [acc_pool.tile([P, BANK], F32, name="acc", tag="acc") for b in range(2)]
+            for a, b in order:
+                mm1(c, banks[b], a, b)
+            h[c] = ring.tile([P, S], F32, name="h", tag="h")
+            for b in range(2):
+                nc.scalar.activation(h[c][:, BANK * b : BANK * (b + 1)], banks[b][:], ACT.Square)
+
+        picked = {}
+
+        def pick(c, which, j0, j1):
+            t = keep.tile([P, (j1 - j0) * P], F32, name="pick%d_%d_%d" % (c, which, j0), align_bytes=64)
+            lst = (pos1_sb, pos2_sb)[which]
+            nc.vector.tensor_copy(t[:], h[c][:].indirect(lst[:, 8 * j0 : 8 * j1]))
+            picked[(c, which, j0)] = t
+
+        z_t = [keep.tile([P, 4, 2, 2 * P], BF16, name="zt%d" % a, align_bytes=64) for a in range(PASSES)]
+
+        def amplitude(c, j0, j1):
+            bank = sum_pool.tile([P, j1 - j0, 2, 64], F32, name="sums", tag="sums")
+            for j in range(j1 - j0):
+                for which in range(2):
+                    nc.tensor.matmul(
+                        bank[:, j, :, :].rearrange("p u m -> p (u m)"),
+                        lhsT=picked[(c, which, j0)][:, j * P : (j + 1) * P],
+                        rhs=perm[:],
+                        start=(which == 0),
+                        stop=(which == 1),
+                        is_transpose=True,
+                    )
+            nc.scalar.activation(z_t[c // 4][:, j0:j1, :, 64 * (c % 4) : 64 * (c % 4 + 1)], bank[:], ACT.Sqrt)
+
+        z_bf = [keep.tile([P, PAIRS, 4], BF16, name="zbf%d" % a, align_bytes=64) for a in range(PASSES)]
+        z_codes = [keep.tile([P, PAIRS], U32, name="zc%d" % a, align_bytes=64) for a in range(PASSES)]
+        z_sc = [keep.tile([P, PAIRS], U8, name="zs%d" % a, align_bytes=64) for a in range(PASSES)]
+
+        def turn_back(a, half, copy):
+            bank = turn_pool.tile([P, 2, 2, P], F32, name="turn", tag="turn")
+            for j in range(2):
+                for u in range(2):
+                    nc.tensor.transpose(bank[:, j, u, :], z_t[a][:, 2 * half + j, u, :].bitcast(F32), ident[:])
+            cols = slice(256 * half, 256 * (half + 1))
+            copy(
+                z_bf[a][:, cols, :].bitcast(F32).rearrange("p (j n) u -> p j n u", j=2),
+                bank[:].rearrange("p j u n -> p j n u"),
+            )
+
+        def quant_z(a, half):
+            cols = slice(256 * half, 256 * (half + 1))
+            nc.vector.quantize_mx(
+                out=z_codes[a][:, cols].bitcast(FP8X4),
+                scales=z_sc[a][:, cols],
+                in_=z_bf[a][:, cols, :].rearrange("p n t -> p (n t)"),
+            )
+
+        def mm2(bank, t, a):
+            nc.tensor.matmul_mx(
+                out=bank[:],
+                lhsT=w2_sb[:, a, 2 * P * t : 2 * P * (t + 1)].bitcast(FP4X4),
+                lhsT_scale=w2_sc[:, a, :].bitcast(U8)[:, P * t : P * (t + 1)],
+                rhs=z_codes[a][:].bitcast(FP8X4),
+                rhs_scale=z_sc[a][:],
+                start=(a == 0),
+                stop=(a == PASSES - 1),
+            )
+
+        gather_tab(0, 0)
+        cast(0, 0)
+        gather_tab(0, 1)
+        nc.vector.tensor_copy(v_sc[:], tab_sc[:].bitcast(U8).indirect(offs_sb[:]))
+        quant_w(0, 0, 1)
+        gather_tab(1, 0)
+        cast(0, 1)
+        quant_w(0, 1, 2)
+        gather_tab(1, 1)
+        energy(0, ((0, 0), (0, 1), (1, 0), (1, 1)))
+        cast(1, 0)
+        cast(1, 1)
+        quant_w(1, 0, 2)
+        cast(2, 0)
+        cast(2, 1)
+        for c in range(TILES - 1):
+            energy(c + 1, ((0, 0), (1, 0), (0, 1), (1, 1)))
+            if c + 3 < TILES:
+                cast(c + 3, 0)
+                cast(c + 3, 1)
+            pick(c, 0, 0, 4)
+            if c + 2 < TILES:
+                quant_w(c + 2, 0, 2)
+            if c == 6:
+                quant_z(0, 0)
+            pick(c, 1, 0, 4)
+            if c == 6:
+                quant_z(0, 1)
+            if c > 0:
+                amplitude(c - 1, 0, 4)
+            if c == 5:
+                turn_back(0, 0, nc.scalar.copy)
+                turn_back(0, 1, nc.scalar.copy)
+        amplitude(TILES - 2, 0, 4)
+        last = TILES - 1
+        scores = [acc_pool.tile([P, BANK], F32, name="acc", tag="acc") for t in range(4)]
+        for t in range(4):
+            mm2(scores[t], t, 0)
+        for half in range(2):
+            pick(last, 0, 2 * half, 2 * half + 2)
+            pick(last, 1, 2 * half, 2 * half + 2)
+            amplitude(last, 2 * half, 2 * half + 2)
+        nc.scalar.activation(warm2[:], z_t[1][:, 3, 1, 255:256], ACT.Sigmoid)
+        for half in range(2):
+            turn_back(1, half, nc.vector.tensor_copy)
+        for half in range(2):
+            quant_z(1, half)
+        for t in range(4):
+            mm2(scores[t], t, 1)
+            res = ring.tile([P, BANK], F32, name="res", tag="res")
+            nc.scalar.activation(res[:], scores[t][:], ACT.Sigmoid, bias=bias[:, t : t + 1])
+            nc.sync.dma_start(out[P * t : P * (t + 1), :], res[:])

@@ -20,7 +20,8 @@ P = 128
 PASSES = 2
 BANK = 512
 TILES = H // P
-CHUNKS = ((0, 1), (1, 1), (2, 1), (3, 1), (4, 2), (6, 2))
+SUM_BANK = {0: 3, 1: 5, 2: 1, 3: 3, 4: 2, 5: 3, 6: 2}
+SCORE_BANK = (0, 1, 4, 5)
 
 
 def tile_list_seismic_arrival_score_kernel(tc, tab_words, tab_scales, offs, pos1, pos2, w1, w2_words, w2_scales, b2, out):
@@ -28,9 +29,7 @@ def tile_list_seismic_arrival_score_kernel(tc, tab_words, tab_scales, offs, pos1
     with ExitStack() as ctx:
         keep = ctx.enter_context(tc.tile_pool(name="keep", bufs=1))
         ring = ctx.enter_context(tc.tile_pool(name="ring", bufs=4))
-        acc_pool = ctx.enter_context(tc.psum_pool(name="acc", bufs=4))
-        sum_pool = ctx.enter_context(tc.psum_pool(name="sums", bufs=2))
-        turn_pool = ctx.enter_context(tc.psum_pool(name="turn", bufs=2))
+        psum = ctx.enter_context(tc.psum_pool(name="psum", bufs=1))
 
         offs_sb = keep.tile([P, S // 16], U16, name="offs_sb")
         pos1_sb = keep.tile([P, PAIRS // 16], U16, name="pos1_sb")
@@ -52,12 +51,11 @@ def tile_list_seismic_arrival_score_kernel(tc, tab_words, tab_scales, offs, pos1
 
         raw = {}
 
-        def load_w1(first, count, a):
-            t = keep.tile([P, 4, count * P], F32, name="raw%d_%d" % (first, a), align_bytes=64)
-            rows = w1[a * 512 : (a + 1) * 512, first * P : (first + count) * P]
+        def load_w1(c, a):
+            t = keep.tile([P, 4, P], F32, name="raw", tag="raw%d_%d" % (c, a), align_bytes=64)
+            rows = w1[a * 512 : (a + 1) * 512, c * P : (c + 1) * P]
             nc.sync.dma_start(t[:], rows.rearrange("(p j) w -> p j w", j=4))
-            for c in range(count):
-                raw[(first + c, a)] = t[:, :, c * P : (c + 1) * P]
+            raw[(c, a)] = t
 
         def load_tab(a):
             nc.sync.dma_start(tab_sb[a][:], tab_words[a].rearrange("p t i -> p (t i)").bitcast(I32))
@@ -68,14 +66,14 @@ def tile_list_seismic_arrival_score_kernel(tc, tab_words, tab_scales, offs, pos1
             for q in range(4):
                 row = 32 * q + 4 * a
                 nc.sync.dma_start(tab_sc[row : row + 4, :], tab_scales[a, 4 * q : 4 * q + 4, :].bitcast(I32))
-        load_w1(0, 1, 0)
+        load_w1(0, 0)
         load_tab(1)
-        load_w1(0, 1, 1)
+        load_w1(0, 1)
         nc.sync.dma_start(pos1_sb[:], pos1)
         nc.sync.dma_start(pos2_sb[:], pos2)
-        for first, count in CHUNKS[1:]:
+        for c in range(1, TILES):
             for a in range(PASSES):
-                load_w1(first, count, a)
+                load_w1(c, a)
         nc.sync.dma_start(w2_sb[:], w2_words.rearrange("a p n -> p a n"))
         for q in range(4):
             nc.sync.dma_start(
@@ -103,8 +101,8 @@ def tile_list_seismic_arrival_score_kernel(tc, tab_words, tab_scales, offs, pos1
 
         def cast(c, a):
             nc.scalar.copy(
-                w_bf[c][:, a, :, :].rearrange("p (g i) t -> p g t i", i=4),
-                raw[(c, a)].rearrange("p t (g i) -> p g t i", i=4),
+                w_bf[c][:, a, :, :].rearrange("p (g i) t -> p g t i", i=2),
+                raw[(c, a)][:].rearrange("p t (g i) -> p g t i", i=2),
             )
 
         def quant_w(c, a0, a1):
@@ -128,7 +126,7 @@ def tile_list_seismic_arrival_score_kernel(tc, tab_words, tab_scales, offs, pos1
         h = {}
 
         def energy(c, order):
-            banks = [acc_pool.tile([P, BANK], F32, name="acc", tag="acc") for b in range(2)]
+            banks = [psum.tile([P, BANK], F32, name="acc", tag="bank%d" % (2 * (c % 3) + b)) for b in range(2)]
             for a, b in order:
                 mm1(c, banks[b], a, b)
             h[c] = ring.tile([P, S], F32, name="h", tag="h")
@@ -137,16 +135,17 @@ def tile_list_seismic_arrival_score_kernel(tc, tab_words, tab_scales, offs, pos1
 
         picked = {}
 
-        def pick(c, which, j0, j1):
-            t = keep.tile([P, (j1 - j0) * P], F32, name="pick%d_%d_%d" % (c, which, j0), align_bytes=64)
+        def pick(c, which, j0, j1, after=None):
+            tag = "pick%d_%d_%d" % (c, which, j0) if after is None else "raw%d_1" % after
+            t = keep.tile([P, (j1 - j0) * P], F32, name="pick", tag=tag, align_bytes=64)
             lst = (pos1_sb, pos2_sb)[which]
             nc.vector.tensor_copy(t[:], h[c][:].indirect(lst[:, 8 * j0 : 8 * j1]))
             picked[(c, which, j0)] = t
 
         z_t = [keep.tile([P, 4, 2, 2 * P], BF16, name="zt%d" % a, align_bytes=64) for a in range(PASSES)]
 
-        def amplitude(c, j0, j1):
-            bank = sum_pool.tile([P, j1 - j0, 2, 64], F32, name="sums", tag="sums")
+        def amplitude(c, j0, j1, where):
+            bank = psum.tile([P, j1 - j0, 2, 64], F32, name="sums", tag="bank%d" % where)
             for j in range(j1 - j0):
                 for which in range(2):
                     nc.tensor.matmul(
@@ -163,19 +162,19 @@ def tile_list_seismic_arrival_score_kernel(tc, tab_words, tab_scales, offs, pos1
         z_codes = [keep.tile([P, PAIRS], U32, name="zc%d" % a, align_bytes=64) for a in range(PASSES)]
         z_sc = [keep.tile([P, PAIRS], U8, name="zs%d" % a, align_bytes=64) for a in range(PASSES)]
 
-        def turn_back(a, half, copy):
-            bank = turn_pool.tile([P, 2, 2, P], F32, name="turn", tag="turn")
-            for j in range(2):
+        def turn_back(a, j0, j1, where, copy):
+            bank = psum.tile([P, j1 - j0, 2, P], F32, name="turn", tag="bank%d" % where)
+            for j in range(j0, j1):
                 for u in range(2):
-                    nc.tensor.transpose(bank[:, j, u, :], z_t[a][:, 2 * half + j, u, :].bitcast(F32), ident[:])
-            cols = slice(256 * half, 256 * (half + 1))
+                    nc.tensor.transpose(bank[:, j - j0, u, :], z_t[a][:, j, u, :].bitcast(F32), ident[:])
+            cols = slice(P * j0, P * j1)
             copy(
-                z_bf[a][:, cols, :].bitcast(F32).rearrange("p (j n) u -> p j n u", j=2),
+                z_bf[a][:, cols, :].bitcast(F32).rearrange("p (j n) u -> p j n u", n=P),
                 bank[:].rearrange("p j u n -> p j n u"),
             )
 
-        def quant_z(a, half):
-            cols = slice(256 * half, 256 * (half + 1))
+        def quant_z(a, j0, j1):
+            cols = slice(P * j0, P * j1)
             nc.vector.quantize_mx(
                 out=z_codes[a][:, cols].bitcast(FP8X4),
                 scales=z_sc[a][:, cols],
@@ -205,41 +204,50 @@ def tile_list_seismic_arrival_score_kernel(tc, tab_words, tab_scales, offs, pos1
         energy(0, ((0, 0), (0, 1), (1, 0), (1, 1)))
         cast(1, 0)
         cast(1, 1)
+        pick(0, 0, 0, 4)
         quant_w(1, 0, 2)
+        pick(0, 1, 0, 4, after=1)
         cast(2, 0)
         cast(2, 1)
-        for c in range(TILES - 1):
+        quant_w(2, 0, 2)
+        energy(1, ((0, 0), (1, 0), (0, 1), (1, 1)))
+        for c in range(1, TILES - 1):
+            if c + 2 < TILES:
+                cast(c + 2, 0)
+                cast(c + 2, 1)
             energy(c + 1, ((0, 0), (1, 0), (0, 1), (1, 1)))
-            if c + 3 < TILES:
-                cast(c + 3, 0)
-                cast(c + 3, 1)
-            pick(c, 0, 0, 4)
+            pick(c, 0, 0, 4, after=2 if c == 1 else None)
             if c + 2 < TILES:
                 quant_w(c + 2, 0, 2)
-            if c == 6:
-                quant_z(0, 0)
-            pick(c, 1, 0, 4)
-            if c == 6:
-                quant_z(0, 1)
-            if c > 0:
-                amplitude(c - 1, 0, 4)
-            if c == 5:
-                turn_back(0, 0, nc.scalar.copy)
-                turn_back(0, 1, nc.scalar.copy)
-        amplitude(TILES - 2, 0, 4)
+            pick(c, 1, 0, 4, after=c + 2 if c + 2 < TILES else None)
+            if c >= 3:
+                amplitude(c - 3, 0, 4, SUM_BANK[c - 3])
         last = TILES - 1
-        scores = [acc_pool.tile([P, BANK], F32, name="acc", tag="acc") for t in range(4)]
+        for half in range(2):
+            turn_back(0, 2 * half, 2 * half + 2, 6 + half, nc.scalar.copy)
+        for c in (4, 5, 6):
+            amplitude(c, 0, 4, SUM_BANK[c])
+        pick(last, 0, 0, 2)
+        pick(last, 1, 0, 2)
+        quant_z(0, 0, 2)
+        pick(last, 0, 2, 3)
+        pick(last, 1, 2, 3)
+        quant_z(0, 2, 4)
+        pick(last, 0, 3, 4)
+        pick(last, 1, 3, 4)
+        scores = [psum.tile([P, BANK], F32, name="score", tag="bank%d" % SCORE_BANK[t]) for t in range(4)]
         for t in range(4):
             mm2(scores[t], t, 0)
-        for half in range(2):
-            pick(last, 0, 2 * half, 2 * half + 2)
-            pick(last, 1, 2 * half, 2 * half + 2)
-            amplitude(last, 2 * half, 2 * half + 2)
+        amplitude(last, 0, 2, 3)
+        amplitude(last, 2, 3, 2)
+        turn_back(1, 0, 2, 6, nc.vector.tensor_copy)
+        amplitude(last, 3, 4, 3)
         nc.scalar.activation(warm2[:], z_t[1][:, 3, 1, 255:256], ACT.Sigmoid)
-        for half in range(2):
-            turn_back(1, half, nc.vector.tensor_copy)
-        for half in range(2):
-            quant_z(1, half)
+        turn_back(1, 2, 3, 7, nc.vector.tensor_copy)
+        quant_z(1, 0, 2)
+        turn_back(1, 3, 4, 2, nc.vector.tensor_copy)
+        quant_z(1, 2, 3)
+        quant_z(1, 3, 4)
         for t in range(4):
             mm2(scores[t], t, 1)
             res = ring.tile([P, BANK], F32, name="res", tag="res")

@@ -20,8 +20,10 @@ P = 128
 PASSES = 2
 BANK = 512
 TILES = H // P
-SUM_BANK = {0: 3, 1: 5, 2: 1, 3: 3, 4: 2, 5: 3, 6: 2}
-SCORE_BANK = (0, 1, 4, 5)
+SUM_BANK = {0: 5, 1: 1, 2: 3, 3: 5, 4: 1, 5: 6, 6: 2}
+LAST_BANK = (7, 3, 6, 2)
+EARLY = 384
+SCORE_BANK = (0, 4, 5, 1)
 
 
 def tile_list_seismic_arrival_score_kernel(tc, tab_words, tab_scales, offs, pos1, pos2, w1, w2_words, w2_scales, b2, out):
@@ -35,7 +37,7 @@ def tile_list_seismic_arrival_score_kernel(tc, tab_words, tab_scales, offs, pos1
         pos1_sb = keep.tile([P, PAIRS // 16], U16, name="pos1_sb")
         pos2_sb = keep.tile([P, PAIRS // 16], U16, name="pos2_sb")
         tab_sb = [keep.tile([P, T], I32, name="tab%d" % a, align_bytes=64) for a in range(PASSES)]
-        tab_sc = keep.tile([P, T // 4], I32, name="tab_sc", align_bytes=64)
+        tab_sc = keep.tile([P, T // 4], I32, name="tab_sc", tag="tab_sc", align_bytes=64)
         w2_sb = keep.tile([P, PASSES, 2 * N], U8, name="w2_sb", align_bytes=64)
         w2_sc = keep.tile([P, PASSES, N // 4], I32, name="w2_sc", align_bytes=64)
         bias = keep.tile([P, N // P], F32, name="bias")
@@ -44,7 +46,8 @@ def tile_list_seismic_arrival_score_kernel(tc, tab_words, tab_scales, offs, pos1
         ident = keep.tile([P, P], F32, name="ident", align_bytes=64)
         perm = keep.tile([P, P], F32, name="perm", align_bytes=64)
 
-        nc.vector.memset(tab_sc[:], 0)
+        nc.vector.memset(tab_sc[:, : T // 8], 0)
+        nc.gpsimd.memset(tab_sc[:, T // 8 :], 0)
         nc.vector.memset(w2_sc[:], 0)
         nc.vector.memset(warm[:, 0:1], 1.0)
         nc.scalar.activation(warm[:, 1:2], warm[:, 0:1], ACT.Sqrt)
@@ -60,17 +63,22 @@ def tile_list_seismic_arrival_score_kernel(tc, tab_words, tab_scales, offs, pos1
         def load_tab(a):
             nc.sync.dma_start(tab_sb[a][:], tab_words[a].rearrange("p t i -> p (t i)").bitcast(I32))
 
-        load_tab(0)
-        nc.sync.dma_start(offs_sb[:], offs)
-        for a in range(PASSES):
-            for q in range(4):
-                row = 32 * q + 4 * a
-                nc.sync.dma_start(tab_sc[row : row + 4, :], tab_scales[a, 4 * q : 4 * q + 4, :].bitcast(I32))
+        def load_tab_scales(i):
+            a, q = divmod(i, 4)
+            row = 32 * q + 4 * a
+            nc.sync.dma_start(tab_sc[row : row + 4, :], tab_scales[a, 4 * q : 4 * q + 4, :].bitcast(I32))
+
         load_w1(0, 0)
-        load_tab(1)
-        load_w1(0, 1)
+        nc.sync.dma_start(offs_sb[:], offs)
         nc.sync.dma_start(pos1_sb[:], pos1)
         nc.sync.dma_start(pos2_sb[:], pos2)
+        for i in range(2):
+            load_tab_scales(i)
+        load_tab(0)
+        for i in range(2, 8):
+            load_tab_scales(i)
+        load_tab(1)
+        load_w1(0, 1)
         for c in range(1, TILES):
             for a in range(PASSES):
                 load_w1(c, a)
@@ -89,10 +97,12 @@ def tile_list_seismic_arrival_score_kernel(tc, tab_words, tab_scales, offs, pos1
             ident[:].rearrange("k (p u e) -> k u p e", u=2, e=2),
         )
 
-        v_codes = [[keep.tile([P, BANK], U32, name="v%d_%d" % (a, b), align_bytes=64) for b in range(2)] for a in range(PASSES)]
+        v_codes = [[None, None], [None, None]]
         v_sc = keep.tile([P, S], U8, name="v_sc", align_bytes=64)
 
         def gather_tab(a, b):
+            tag = "raw0_1" if (a, b) == (1, 1) else "v%d_%d" % (a, b)
+            v_codes[a][b] = keep.tile([P, BANK], U32, name="v", tag=tag, align_bytes=64)
             nc.vector.tensor_copy(v_codes[a][b][:], tab_sb[a][:].bitcast(U32).indirect(offs_sb[:, 32 * b : 32 * (b + 1)]))
 
         w_bf = [keep.tile([P, PASSES, P, 4], BF16, name="wbf%d" % c, align_bytes=64) for c in range(TILES)]
@@ -159,8 +169,13 @@ def tile_list_seismic_arrival_score_kernel(tc, tab_words, tab_scales, offs, pos1
             nc.scalar.activation(z_t[c // 4][:, j0:j1, :, 64 * (c % 4) : 64 * (c % 4 + 1)], bank[:], ACT.Sqrt)
 
         z_bf = [keep.tile([P, PAIRS, 4], BF16, name="zbf%d" % a, align_bytes=64) for a in range(PASSES)]
-        z_codes = [keep.tile([P, PAIRS], U32, name="zc%d" % a, align_bytes=64) for a in range(PASSES)]
-        z_sc = [keep.tile([P, PAIRS], U8, name="zs%d" % a, align_bytes=64) for a in range(PASSES)]
+        z_codes = keep.tile([P, PASSES * PAIRS], U32, name="z_codes", align_bytes=64)
+        z_sc = keep.tile([P, PASSES * PAIRS], U8, name="z_sc", align_bytes=64)
+
+        def z_col(a, j):
+            if a == 0:
+                return EARLY + P * j
+            return P * j if j < 3 else EARLY + PAIRS
 
         def turn_back(a, j0, j1, where, copy):
             bank = psum.tile([P, j1 - j0, 2, P], F32, name="turn", tag="bank%d" % where)
@@ -175,19 +190,21 @@ def tile_list_seismic_arrival_score_kernel(tc, tab_words, tab_scales, offs, pos1
 
         def quant_z(a, j0, j1):
             cols = slice(P * j0, P * j1)
+            at = slice(z_col(a, j0), z_col(a, j0) + P * (j1 - j0))
             nc.vector.quantize_mx(
-                out=z_codes[a][:, cols].bitcast(FP8X4),
-                scales=z_sc[a][:, cols],
+                out=z_codes[:, at].bitcast(FP8X4),
+                scales=z_sc[:, at],
                 in_=z_bf[a][:, cols, :].rearrange("p n t -> p (n t)"),
             )
 
-        def mm2(bank, t, a):
+        def mm2(dst, t, a, j, width):
+            at = slice(z_col(a, j), z_col(a, j) + width)
             nc.tensor.matmul_mx(
-                out=bank[:],
+                out=dst,
                 lhsT=w2_sb[:, a, 2 * P * t : 2 * P * (t + 1)].bitcast(FP4X4),
                 lhsT_scale=w2_sc[:, a, :].bitcast(U8)[:, P * t : P * (t + 1)],
-                rhs=z_codes[a][:].bitcast(FP8X4),
-                rhs_scale=z_sc[a][:],
+                rhs=z_codes[:, at].bitcast(FP8X4),
+                rhs_scale=z_sc[:, at],
                 start=(a == 0),
                 stop=(a == PASSES - 1),
             )
@@ -204,52 +221,62 @@ def tile_list_seismic_arrival_score_kernel(tc, tab_words, tab_scales, offs, pos1
         energy(0, ((0, 0), (0, 1), (1, 0), (1, 1)))
         cast(1, 0)
         cast(1, 1)
-        pick(0, 0, 0, 4)
         quant_w(1, 0, 2)
-        pick(0, 1, 0, 4, after=1)
         cast(2, 0)
         cast(2, 1)
-        quant_w(2, 0, 2)
         energy(1, ((0, 0), (1, 0), (0, 1), (1, 1)))
-        for c in range(1, TILES - 1):
-            if c + 2 < TILES:
-                cast(c + 2, 0)
-                cast(c + 2, 1)
-            energy(c + 1, ((0, 0), (1, 0), (0, 1), (1, 1)))
-            pick(c, 0, 0, 4, after=2 if c == 1 else None)
+        pick(0, 0, 0, 4, after=1)
+        quant_w(2, 0, 2)
+        pick(0, 1, 0, 4, after=2)
+        cast(3, 0)
+        cast(3, 1)
+        for c in range(1, TILES - 2):
             if c + 2 < TILES:
                 quant_w(c + 2, 0, 2)
-            pick(c, 1, 0, 4, after=c + 2 if c + 2 < TILES else None)
-            if c >= 3:
-                amplitude(c - 3, 0, 4, SUM_BANK[c - 3])
+            energy(c + 1, ((0, 0), (1, 0), (0, 1), (1, 1)))
+            if c + 3 < TILES:
+                cast(c + 3, 0)
+                cast(c + 3, 1)
+            pick(c, 0, 0, 4, after=c + 2 if c + 2 < TILES else None)
+            pick(c, 1, 0, 4)
+            amplitude(c - 1, 0, 4, SUM_BANK[c - 1])
         last = TILES - 1
         for half in range(2):
             turn_back(0, 2 * half, 2 * half + 2, 6 + half, nc.scalar.copy)
-        for c in (4, 5, 6):
-            amplitude(c, 0, 4, SUM_BANK[c])
-        pick(last, 0, 0, 2)
-        pick(last, 1, 0, 2)
-        quant_z(0, 0, 2)
-        pick(last, 0, 2, 3)
-        pick(last, 1, 2, 3)
-        quant_z(0, 2, 4)
-        pick(last, 0, 3, 4)
-        pick(last, 1, 3, 4)
+        energy(last, ((0, 0), (1, 0), (0, 1), (1, 1)))
+        pick(6, 0, 0, 4)
+        quant_z(0, 0, 4)
+        pick(6, 1, 0, 4)
+        amplitude(5, 0, 4, SUM_BANK[5])
         scores = [psum.tile([P, BANK], F32, name="score", tag="bank%d" % SCORE_BANK[t]) for t in range(4)]
         for t in range(4):
-            mm2(scores[t], t, 0)
-        amplitude(last, 0, 2, 3)
-        amplitude(last, 2, 3, 2)
-        turn_back(1, 0, 2, 6, nc.vector.tensor_copy)
-        amplitude(last, 3, 4, 3)
+            mm2(scores[t][:], t, 0, 0, BANK)
+        amplitude(6, 0, 4, SUM_BANK[6])
+        for j in range(4):
+            pick(last, 0, j, j + 1)
+            pick(last, 1, j, j + 1)
+        for j in range(4):
+            amplitude(last, j, j + 1, LAST_BANK[j])
+            if j > 0:
+                turn_back(1, j - 1, j, LAST_BANK[j - 1], nc.vector.tensor_copy)
         nc.scalar.activation(warm2[:], z_t[1][:, 3, 1, 255:256], ACT.Sigmoid)
-        turn_back(1, 2, 3, 7, nc.vector.tensor_copy)
         quant_z(1, 0, 2)
-        turn_back(1, 3, 4, 2, nc.vector.tensor_copy)
         quant_z(1, 2, 3)
-        quant_z(1, 3, 4)
+        turn_back(1, 3, 4, LAST_BANK[3], nc.vector.tensor_copy)
         for t in range(4):
-            mm2(scores[t], t, 1)
-            res = ring.tile([P, BANK], F32, name="res", tag="res")
-            nc.scalar.activation(res[:], scores[t][:], ACT.Sigmoid, bias=bias[:, t : t + 1])
-            nc.sync.dma_start(out[P * t : P * (t + 1), :], res[:])
+            mm2(scores[t][:], t, 1, 0, BANK)
+        quant_z(1, 3, 4)
+        late = [psum.tile([P, 2, P], F32, name="late", tag="bank%d" % LAST_BANK[g]) for g in range(2)]
+        for t in range(4):
+            for a in range(PASSES):
+                mm2(late[t // 2][:, t % 2, :], t, a, 3, P)
+        for t in range(4):
+            res = ring.tile([P, EARLY], F32, name="res", tag="res")
+            nc.scalar.activation(res[:], scores[t][:, :EARLY], ACT.Sigmoid, bias=bias[:, t : t + 1])
+            nc.sync.dma_start(out[P * t : P * (t + 1), :EARLY], res[:])
+        for g in range(2):
+            res = ring.tile([P, 2, P], F32, name="res_late", tag="res_late")
+            for i in range(2):
+                t = 2 * g + i
+                nc.scalar.activation(res[:, i, :], late[g][:, i, :], ACT.Sigmoid, bias=bias[:, t : t + 1])
+            nc.sync.dma_start(out[2 * P * g : 2 * P * (g + 1), EARLY:].rearrange("(t p) n -> p t n", p=P), res[:])

@@ -17,13 +17,24 @@ FP4X4 = mybir.dt.float4_e2m1fn_x4
 ACT = mybir.ActivationFunctionType
 
 P = 128
+PACK = 4
+K_PASS = P * PACK
 PASSES = 2
 BANK = 512
+HALVES = S // BANK
 TILES = H // P
-SUM_BANK = {0: 5, 1: 1, 2: 3, 3: 5, 4: 1, 5: 6, 6: 2}
+TILES_PER_PASS = K_PASS // P
+GROUPS = PAIRS // P
+CLASS_TILES = N // P
+LIST_COLS = P // 16
+
+EARLY = (GROUPS - 1) * P
+
+SUM_BANK = (5, 1, 3, 5, 1, 6, 2)
+TURN_BANK = (6, 7)
 LAST_BANK = (7, 3, 6, 2)
-EARLY = 384
 SCORE_BANK = (0, 4, 5, 1)
+LATE_BANK = (7, 3)
 
 
 def tile_list_seismic_arrival_score_kernel(tc, tab_words, tab_scales, offs, pos1, pos2, w1, w2_words, w2_scales, b2, out):
@@ -37,36 +48,34 @@ def tile_list_seismic_arrival_score_kernel(tc, tab_words, tab_scales, offs, pos1
         pos1_sb = keep.tile([P, PAIRS // 16], U16, name="pos1_sb")
         pos2_sb = keep.tile([P, PAIRS // 16], U16, name="pos2_sb")
         tab_sb = [keep.tile([P, T], I32, name="tab%d" % a, align_bytes=64) for a in range(PASSES)]
-        tab_sc = keep.tile([P, T // 4], I32, name="tab_sc", tag="tab_sc", align_bytes=64)
+        tab_sc = keep.tile([P, T // 4], I32, name="tab_sc", align_bytes=64)
         w2_sb = keep.tile([P, PASSES, 2 * N], U8, name="w2_sb", align_bytes=64)
         w2_sc = keep.tile([P, PASSES, N // 4], I32, name="w2_sc", align_bytes=64)
-        bias = keep.tile([P, N // P], F32, name="bias")
-        warm = keep.tile([P, 2], F32, name="warm")
-        warm2 = keep.tile([P, 1], F32, name="warm2")
+        bias = keep.tile([P, CLASS_TILES], F32, name="bias")
+        zero = keep.tile([P, 1], F32, name="zero")
+        no_bias = keep.tile([P, 1], F32, name="no_bias")
         ident = keep.tile([P, P], F32, name="ident", align_bytes=64)
         perm = keep.tile([P, P], F32, name="perm", align_bytes=64)
 
         nc.vector.memset(tab_sc[:, : T // 8], 0)
         nc.gpsimd.memset(tab_sc[:, T // 8 :], 0)
         nc.vector.memset(w2_sc[:], 0)
-        nc.vector.memset(warm[:, 0:1], 1.0)
-        nc.scalar.activation(warm[:, 1:2], warm[:, 0:1], ACT.Sqrt)
+        nc.vector.memset(zero[:], 0.0)
+        nc.scalar.activation(no_bias[:], zero[:], ACT.Sqrt)
 
         raw = {}
 
         def load_w1(c, a):
-            t = keep.tile([P, 4, P], F32, name="raw", tag="raw%d_%d" % (c, a), align_bytes=64)
-            rows = w1[a * 512 : (a + 1) * 512, c * P : (c + 1) * P]
-            nc.sync.dma_start(t[:], rows.rearrange("(p j) w -> p j w", j=4))
-            raw[(c, a)] = t
+            raw[(c, a)] = keep.tile([P, PACK, P], F32, name="raw", tag="raw%d_%d" % (c, a), align_bytes=64)
+            rows = w1[a * K_PASS : (a + 1) * K_PASS, c * P : (c + 1) * P]
+            nc.sync.dma_start(raw[(c, a)][:], rows.rearrange("(p t) m -> p t m", t=PACK))
 
         def load_tab(a):
             nc.sync.dma_start(tab_sb[a][:], tab_words[a].rearrange("p t i -> p (t i)").bitcast(I32))
 
         def load_tab_scales(i):
-            a, q = divmod(i, 4)
-            row = 32 * q + 4 * a
-            nc.sync.dma_start(tab_sc[row : row + 4, :], tab_scales[a, 4 * q : 4 * q + 4, :].bitcast(I32))
+            s, a = divmod(i, PASSES)
+            nc.sync.dma_start(tab_sc[4 * a + s : P : 32, :], tab_scales[a, s:16:4, :].bitcast(I32))
 
         load_w1(0, 0)
         nc.sync.dma_start(offs_sb[:], offs)
@@ -86,7 +95,7 @@ def tile_list_seismic_arrival_score_kernel(tc, tab_words, tab_scales, offs, pos1
         for q in range(4):
             nc.sync.dma_start(
                 w2_sc[32 * q : 32 * q + 4, :, :],
-                w2_scales[:, 4 * q : 4 * q + 4, :].bitcast(I32).rearrange("a r n -> r a n"),
+                w2_scales[:, 4 * q : 4 * q + 4, :].bitcast(I32).rearrange("a g n -> g a n"),
             )
         with nc.allow_non_contiguous_dma(reason="one bias value a partition"):
             nc.sync.dma_start(bias[:], b2.rearrange("(t p) -> p t", p=P))
@@ -97,65 +106,65 @@ def tile_list_seismic_arrival_score_kernel(tc, tab_words, tab_scales, offs, pos1
             ident[:].rearrange("k (p u e) -> k u p e", u=2, e=2),
         )
 
-        v_codes = [[None, None], [None, None]]
+        v_codes = {}
         v_sc = keep.tile([P, S], U8, name="v_sc", align_bytes=64)
 
         def gather_tab(a, b):
-            tag = "raw0_1" if (a, b) == (1, 1) else "v%d_%d" % (a, b)
-            v_codes[a][b] = keep.tile([P, BANK], U32, name="v", tag=tag, align_bytes=64)
-            nc.vector.tensor_copy(v_codes[a][b][:], tab_sb[a][:].bitcast(U32).indirect(offs_sb[:, 32 * b : 32 * (b + 1)]))
+            tag = "raw0_1" if (a, b) == (PASSES - 1, HALVES - 1) else "v%d_%d" % (a, b)
+            v_codes[(a, b)] = keep.tile([P, BANK], U32, name="v", tag=tag, align_bytes=64)
+            entries = offs_sb[:, BANK // 16 * b : BANK // 16 * (b + 1)]
+            nc.vector.tensor_copy(v_codes[(a, b)][:], tab_sb[a][:].bitcast(U32).indirect(entries))
 
-        w_bf = [keep.tile([P, PASSES, P, 4], BF16, name="wbf%d" % c, align_bytes=64) for c in range(TILES)]
+        w_bf = [keep.tile([P, PASSES, P, PACK], BF16, name="wbf%d" % c, align_bytes=64) for c in range(TILES)]
         w_codes = [keep.tile([P, PASSES, P], U32, name="wc%d" % c, align_bytes=64) for c in range(TILES)]
         w_sc = [keep.tile([P, PASSES, P], U8, name="ws%d" % c, align_bytes=64) for c in range(TILES)]
 
-        def cast(c, a):
+        def round_w1(c, a):
             nc.scalar.copy(
                 w_bf[c][:, a, :, :].rearrange("p (g i) t -> p g t i", i=2),
                 raw[(c, a)][:].rearrange("p t (g i) -> p g t i", i=2),
             )
 
-        def quant_w(c, a0, a1):
+        def quantise_w1(c, a0, a1):
             nc.vector.quantize_mx(
                 out=w_codes[c][:, a0:a1, :].rearrange("p a m -> p (a m)").bitcast(FP8X4),
                 scales=w_sc[c][:, a0:a1, :].rearrange("p a m -> p (a m)"),
                 in_=w_bf[c][:, a0:a1, :, :].rearrange("p a m t -> p (a m t)"),
             )
 
-        def mm1(c, bank, a, b):
-            nc.tensor.matmul_mx(
-                out=bank[:],
-                lhsT=w_codes[c][:, a, :].bitcast(FP8X4),
-                lhsT_scale=w_sc[c][:, a, :],
-                rhs=v_codes[a][b][:].bitcast(FP8X4),
-                rhs_scale=v_sc[4 * a : P, BANK * b : BANK * (b + 1)],
-                start=(a == 0),
-                stop=(a == PASSES - 1),
-            )
-
         h = {}
 
-        def energy(c, order):
-            banks = [psum.tile([P, BANK], F32, name="acc", tag="bank%d" % (2 * (c % 3) + b)) for b in range(2)]
+        def energy(c):
+            banks = [psum.tile([P, BANK], F32, name="acc", tag="bank%d" % (2 * (c % 3) + b)) for b in range(HALVES)]
+            order = [(a, b) for a in range(PASSES) for b in range(HALVES)]
+            if c > 0:
+                order = [(a, b) for b in range(HALVES) for a in range(PASSES)]
             for a, b in order:
-                mm1(c, banks[b], a, b)
+                nc.tensor.matmul_mx(
+                    out=banks[b][:],
+                    lhsT=w_codes[c][:, a, :].bitcast(FP8X4),
+                    lhsT_scale=w_sc[c][:, a, :],
+                    rhs=v_codes[(a, b)][:].bitcast(FP8X4),
+                    rhs_scale=v_sc[4 * a : P, BANK * b : BANK * (b + 1)],
+                    start=(a == 0),
+                    stop=(a == PASSES - 1),
+                )
             h[c] = ring.tile([P, S], F32, name="h", tag="h")
-            for b in range(2):
-                nc.scalar.activation(h[c][:, BANK * b : BANK * (b + 1)], banks[b][:], ACT.Square)
+            for b in range(HALVES):
+                nc.scalar.activation(h[c][:, BANK * b : BANK * (b + 1)], banks[b][:], ACT.Square, bias=no_bias[:])
 
         picked = {}
 
         def pick(c, which, j0, j1, after=None):
             tag = "pick%d_%d_%d" % (c, which, j0) if after is None else "raw%d_1" % after
-            t = keep.tile([P, (j1 - j0) * P], F32, name="pick", tag=tag, align_bytes=64)
-            lst = (pos1_sb, pos2_sb)[which]
-            nc.vector.tensor_copy(t[:], h[c][:].indirect(lst[:, 8 * j0 : 8 * j1]))
-            picked[(c, which, j0)] = t
+            picked[(c, which, j0)] = keep.tile([P, (j1 - j0) * P], F32, name="pick", tag=tag, align_bytes=64)
+            entries = (pos1_sb, pos2_sb)[which][:, LIST_COLS * j0 : LIST_COLS * j1]
+            nc.vector.tensor_copy(picked[(c, which, j0)][:], h[c][:].indirect(entries))
 
-        z_t = [keep.tile([P, 4, 2, 2 * P], BF16, name="zt%d" % a, align_bytes=64) for a in range(PASSES)]
+        z_t = [keep.tile([P, GROUPS, 2, 2 * P], BF16, name="zt%d" % a, align_bytes=64) for a in range(PASSES)]
 
-        def amplitude(c, j0, j1, where):
-            bank = psum.tile([P, j1 - j0, 2, 64], F32, name="sums", tag="bank%d" % where)
+        def amplitude(c, j0, j1, bank_no):
+            bank = psum.tile([P, j1 - j0, 2, P // 2], F32, name="sums", tag="bank%d" % bank_no)
             for j in range(j1 - j0):
                 for which in range(2):
                     nc.tensor.matmul(
@@ -166,38 +175,37 @@ def tile_list_seismic_arrival_score_kernel(tc, tab_words, tab_scales, offs, pos1
                         stop=(which == 1),
                         is_transpose=True,
                     )
-            nc.scalar.activation(z_t[c // 4][:, j0:j1, :, 64 * (c % 4) : 64 * (c % 4 + 1)], bank[:], ACT.Sqrt)
+            a, place = divmod(c, TILES_PER_PASS)
+            nc.scalar.activation(z_t[a][:, j0:j1, :, P // 2 * place : P // 2 * (place + 1)], bank[:], ACT.Sqrt)
 
-        z_bf = [keep.tile([P, PAIRS, 4], BF16, name="zbf%d" % a, align_bytes=64) for a in range(PASSES)]
+        z_bf = [keep.tile([P, PAIRS, PACK], BF16, name="zbf%d" % a, align_bytes=64) for a in range(PASSES)]
         z_codes = keep.tile([P, PASSES * PAIRS], U32, name="z_codes", align_bytes=64)
         z_sc = keep.tile([P, PASSES * PAIRS], U8, name="z_sc", align_bytes=64)
 
         def z_col(a, j):
             if a == 0:
                 return EARLY + P * j
-            return P * j if j < 3 else EARLY + PAIRS
+            return P * j if j < GROUPS - 1 else EARLY + PAIRS
 
-        def turn_back(a, j0, j1, where, copy):
-            bank = psum.tile([P, j1 - j0, 2, P], F32, name="turn", tag="bank%d" % where)
+        def turn_back(a, j0, j1, bank_no, copy):
+            bank = psum.tile([P, j1 - j0, 2, P], F32, name="turn", tag="bank%d" % bank_no)
             for j in range(j0, j1):
                 for u in range(2):
                     nc.tensor.transpose(bank[:, j - j0, u, :], z_t[a][:, j, u, :].bitcast(F32), ident[:])
-            cols = slice(P * j0, P * j1)
             copy(
-                z_bf[a][:, cols, :].bitcast(F32).rearrange("p (j n) u -> p j n u", n=P),
+                z_bf[a][:, P * j0 : P * j1, :].bitcast(F32).rearrange("p (j n) u -> p j n u", n=P),
                 bank[:].rearrange("p j u n -> p j n u"),
             )
 
-        def quant_z(a, j0, j1):
-            cols = slice(P * j0, P * j1)
+        def quantise_z(a, j0, j1):
             at = slice(z_col(a, j0), z_col(a, j0) + P * (j1 - j0))
             nc.vector.quantize_mx(
                 out=z_codes[:, at].bitcast(FP8X4),
                 scales=z_sc[:, at],
-                in_=z_bf[a][:, cols, :].rearrange("p n t -> p (n t)"),
+                in_=z_bf[a][:, P * j0 : P * j1, :].rearrange("p n t -> p (n t)"),
             )
 
-        def mm2(dst, t, a, j, width):
+        def score_pass(dst, t, a, j, width):
             at = slice(z_col(a, j), z_col(a, j) + width)
             nc.tensor.matmul_mx(
                 out=dst,
@@ -210,73 +218,76 @@ def tile_list_seismic_arrival_score_kernel(tc, tab_words, tab_scales, offs, pos1
             )
 
         gather_tab(0, 0)
-        cast(0, 0)
+        round_w1(0, 0)
         gather_tab(0, 1)
         nc.vector.tensor_copy(v_sc[:], tab_sc[:].bitcast(U8).indirect(offs_sb[:]))
-        quant_w(0, 0, 1)
+        quantise_w1(0, 0, 1)
         gather_tab(1, 0)
-        cast(0, 1)
-        quant_w(0, 1, 2)
+        round_w1(0, 1)
+        quantise_w1(0, 1, 2)
         gather_tab(1, 1)
-        energy(0, ((0, 0), (0, 1), (1, 0), (1, 1)))
-        cast(1, 0)
-        cast(1, 1)
-        quant_w(1, 0, 2)
-        cast(2, 0)
-        cast(2, 1)
-        energy(1, ((0, 0), (1, 0), (0, 1), (1, 1)))
-        pick(0, 0, 0, 4, after=1)
-        quant_w(2, 0, 2)
-        pick(0, 1, 0, 4, after=2)
-        cast(3, 0)
-        cast(3, 1)
-        for c in range(1, TILES - 2):
-            if c + 2 < TILES:
-                quant_w(c + 2, 0, 2)
-            energy(c + 1, ((0, 0), (1, 0), (0, 1), (1, 1)))
-            if c + 3 < TILES:
-                cast(c + 3, 0)
-                cast(c + 3, 1)
-            pick(c, 0, 0, 4, after=c + 2 if c + 2 < TILES else None)
-            pick(c, 1, 0, 4)
-            amplitude(c - 1, 0, 4, SUM_BANK[c - 1])
+        energy(0)
+
+        for a in range(PASSES):
+            round_w1(1, a)
+        quantise_w1(1, 0, PASSES)
+        for a in range(PASSES):
+            round_w1(2, a)
+        energy(1)
+        pick(0, 0, 0, GROUPS, after=1)
+        quantise_w1(2, 0, PASSES)
+        pick(0, 1, 0, GROUPS, after=2)
+        for a in range(PASSES):
+            round_w1(3, a)
+
         last = TILES - 1
+        for c in range(1, last - 1):
+            quantise_w1(c + 2, 0, PASSES)
+            energy(c + 1)
+            if c + 3 <= last:
+                for a in range(PASSES):
+                    round_w1(c + 3, a)
+            pick(c, 0, 0, GROUPS, after=c + 2)
+            pick(c, 1, 0, GROUPS)
+            amplitude(c - 1, 0, GROUPS, SUM_BANK[c - 1])
+
         for half in range(2):
-            turn_back(0, 2 * half, 2 * half + 2, 6 + half, nc.scalar.copy)
-        energy(last, ((0, 0), (1, 0), (0, 1), (1, 1)))
-        pick(6, 0, 0, 4)
-        quant_z(0, 0, 4)
-        pick(6, 1, 0, 4)
-        amplitude(5, 0, 4, SUM_BANK[5])
-        scores = [psum.tile([P, BANK], F32, name="score", tag="bank%d" % SCORE_BANK[t]) for t in range(4)]
-        for t in range(4):
-            mm2(scores[t][:], t, 0, 0, BANK)
-        amplitude(6, 0, 4, SUM_BANK[6])
-        for j in range(4):
+            turn_back(0, 2 * half, 2 * half + 2, TURN_BANK[half], nc.scalar.copy)
+        energy(last)
+        pick(last - 1, 0, 0, GROUPS)
+        quantise_z(0, 0, GROUPS)
+        pick(last - 1, 1, 0, GROUPS)
+        amplitude(last - 2, 0, GROUPS, SUM_BANK[last - 2])
+        scores = [psum.tile([P, BANK], F32, name="score", tag="bank%d" % SCORE_BANK[t]) for t in range(CLASS_TILES)]
+        for t in range(CLASS_TILES):
+            score_pass(scores[t][:], t, 0, 0, BANK)
+        amplitude(last - 1, 0, GROUPS, SUM_BANK[last - 1])
+
+        for j in range(GROUPS):
             pick(last, 0, j, j + 1)
             pick(last, 1, j, j + 1)
-        for j in range(4):
+        for j in range(GROUPS):
             amplitude(last, j, j + 1, LAST_BANK[j])
             if j > 0:
                 turn_back(1, j - 1, j, LAST_BANK[j - 1], nc.vector.tensor_copy)
-        nc.scalar.activation(warm2[:], z_t[1][:, 3, 1, 255:256], ACT.Sigmoid)
-        quant_z(1, 0, 2)
-        quant_z(1, 2, 3)
-        turn_back(1, 3, 4, LAST_BANK[3], nc.vector.tensor_copy)
-        for t in range(4):
-            mm2(scores[t][:], t, 1, 0, BANK)
-        quant_z(1, 3, 4)
-        late = [psum.tile([P, 2, P], F32, name="late", tag="bank%d" % LAST_BANK[g]) for g in range(2)]
-        for t in range(4):
+        quantise_z(1, 0, 2)
+        quantise_z(1, 2, GROUPS - 1)
+        turn_back(1, GROUPS - 1, GROUPS, LAST_BANK[GROUPS - 1], nc.vector.tensor_copy)
+        for t in range(CLASS_TILES):
+            score_pass(scores[t][:], t, 1, 0, BANK)
+        quantise_z(1, GROUPS - 1, GROUPS)
+        late = [psum.tile([P, 2, P], F32, name="late", tag="bank%d" % bank_no) for bank_no in LATE_BANK]
+        for t in range(CLASS_TILES):
             for a in range(PASSES):
-                mm2(late[t // 2][:, t % 2, :], t, a, 3, P)
-        for t in range(4):
+                score_pass(late[t // 2][:, t % 2, :], t, a, GROUPS - 1, P)
+
+        for t in range(CLASS_TILES):
             res = ring.tile([P, EARLY], F32, name="res", tag="res")
             nc.scalar.activation(res[:], scores[t][:, :EARLY], ACT.Sigmoid, bias=bias[:, t : t + 1])
             nc.sync.dma_start(out[P * t : P * (t + 1), :EARLY], res[:])
-        for g in range(2):
-            res = ring.tile([P, 2, P], F32, name="res_late", tag="res_late")
+        for g in range(len(late)):
+            res_late = ring.tile([P, 2, P], F32, name="res_late", tag="res_late")
             for i in range(2):
                 t = 2 * g + i
-                nc.scalar.activation(res[:, i, :], late[g][:, i, :], ACT.Sigmoid, bias=bias[:, t : t + 1])
-            nc.sync.dma_start(out[2 * P * g : 2 * P * (g + 1), EARLY:].rearrange("(t p) n -> p t n", p=P), res[:])
+                nc.scalar.activation(res_late[:, i, :], late[g][:, i, :], ACT.Sigmoid, bias=bias[:, t : t + 1])
+            nc.sync.dma_start(out[2 * P * g : 2 * P * (g + 1), EARLY:].rearrange("(t p) n -> p t n", p=P), res_late[:])

@@ -1,7 +1,6 @@
 from contextlib import ExitStack
 
 import concourse.mybir as mybir
-from concourse.masks import make_identity
 
 K, H, N, T, S, PAIRS = 1024, 1024, 512, 4096, 1024, 512
 FLOPS = 2 * K * H * S + 2 * H * N * PAIRS
@@ -15,6 +14,7 @@ U8 = mybir.dt.uint8
 FP8X4 = mybir.dt.float8_e4m3fn_x4
 FP4X4 = mybir.dt.float4_e2m1fn_x4
 ACT = mybir.ActivationFunctionType
+ADD = mybir.AluOpType.add
 
 P = 128
 PACK = 4
@@ -23,25 +23,13 @@ PASSES = 2
 BANK = 512
 HALVES = S // BANK
 TILES = H // P
-TILES_PER_PASS = K_PASS // P
-GROUPS = PAIRS // P
 CLASS_TILES = N // P
-LIST_COLS = P // 16
-
-EARLY = (GROUPS - 1) * P
-
-SUM_BANK = (5, 1, 3, 5, 1, 6, 2)
-TURN_BANK = (6, 7)
-LAST_BANK = (7, 3, 6, 2)
-SCORE_BANK = (0, 4, 5, 1)
-LATE_BANK = (7, 3)
 
 
 def tile_list_seismic_arrival_score_kernel(tc, tab_words, tab_scales, offs, pos1, pos2, w1, w2_words, w2_scales, b2, out):
     nc = tc.nc
     with ExitStack() as ctx:
         keep = ctx.enter_context(tc.tile_pool(name="keep", bufs=1))
-        ring = ctx.enter_context(tc.tile_pool(name="ring", bufs=4))
         psum = ctx.enter_context(tc.psum_pool(name="psum", bufs=1))
 
         offs_sb = keep.tile([P, S // 16], U16, name="offs_sb")
@@ -54,8 +42,6 @@ def tile_list_seismic_arrival_score_kernel(tc, tab_words, tab_scales, offs, pos1
         bias = keep.tile([P, CLASS_TILES], F32, name="bias")
         zero = keep.tile([P, 1], F32, name="zero")
         no_bias = keep.tile([P, 1], F32, name="no_bias")
-        ident = keep.tile([P, P], F32, name="ident", align_bytes=64)
-        perm = keep.tile([P, P], F32, name="perm", align_bytes=64)
 
         nc.vector.memset(tab_sc[:, : T // 8], 0)
         nc.gpsimd.memset(tab_sc[:, T // 8 :], 0)
@@ -65,10 +51,10 @@ def tile_list_seismic_arrival_score_kernel(tc, tab_words, tab_scales, offs, pos1
 
         raw = {}
 
-        def load_w1(c, a):
-            raw[(c, a)] = keep.tile([P, PACK, P], F32, name="raw", tag="raw%d_%d" % (c, a), align_bytes=64)
-            rows = w1[a * K_PASS : (a + 1) * K_PASS, c * P : (c + 1) * P]
-            nc.sync.dma_start(raw[(c, a)][:], rows.rearrange("(p t) m -> p t m", t=PACK))
+        def load_w1(a, b):
+            raw[(a, b)] = keep.tile([P, PACK, K_PASS], F32, name="raw%d_%d" % (a, b), align_bytes=64)
+            rows = w1[a * K_PASS : (a + 1) * K_PASS, b * K_PASS : (b + 1) * K_PASS]
+            nc.sync.dma_start(raw[(a, b)][:], rows.rearrange("(p t) m -> p t m", t=PACK))
 
         def load_tab(a):
             nc.sync.dma_start(tab_sb[a][:], tab_words[a].rearrange("p t i -> p (t i)").bitcast(I32))
@@ -87,10 +73,9 @@ def tile_list_seismic_arrival_score_kernel(tc, tab_words, tab_scales, offs, pos1
         for i in range(2, 8):
             load_tab_scales(i)
         load_tab(1)
+        load_w1(1, 0)
         load_w1(0, 1)
-        for c in range(1, TILES):
-            for a in range(PASSES):
-                load_w1(c, a)
+        load_w1(1, 1)
         nc.sync.dma_start(w2_sb[:], w2_words.rearrange("a p n -> p a n"))
         for q in range(4):
             nc.sync.dma_start(
@@ -100,194 +85,189 @@ def tile_list_seismic_arrival_score_kernel(tc, tab_words, tab_scales, offs, pos1
         with nc.allow_non_contiguous_dma(reason="one bias value a partition"):
             nc.sync.dma_start(bias[:], b2.rearrange("(t p) -> p t", p=P))
 
-        make_identity(nc, ident[:])
-        nc.vector.tensor_copy(
-            perm[:].rearrange("k (u p e) -> k u p e", u=2, e=2),
-            ident[:].rearrange("k (p u e) -> k u p e", u=2, e=2),
-        )
-
         v_codes = {}
         v_sc = keep.tile([P, S], U8, name="v_sc", align_bytes=64)
 
-        def gather_tab(a, b):
-            tag = "raw0_1" if (a, b) == (PASSES - 1, HALVES - 1) else "v%d_%d" % (a, b)
-            v_codes[(a, b)] = keep.tile([P, BANK], U32, name="v", tag=tag, align_bytes=64)
-            entries = offs_sb[:, BANK // 16 * b : BANK // 16 * (b + 1)]
-            nc.vector.tensor_copy(v_codes[(a, b)][:], tab_sb[a][:].bitcast(U32).indirect(entries))
+        def gather_tab(a, half):
+            v_codes[(a, half)] = keep.tile([P, BANK], U32, name="v%d_%d" % (a, half), align_bytes=64)
+            entries = offs_sb[:, BANK // 16 * half : BANK // 16 * (half + 1)]
+            nc.vector.tensor_copy(v_codes[(a, half)][:], tab_sb[a][:].bitcast(U32).indirect(entries))
 
-        w_bf = [keep.tile([P, PASSES, P, PACK], BF16, name="wbf%d" % c, align_bytes=64) for c in range(TILES)]
-        w_codes = [keep.tile([P, PASSES, P], U32, name="wc%d" % c, align_bytes=64) for c in range(TILES)]
-        w_sc = [keep.tile([P, PASSES, P], U8, name="ws%d" % c, align_bytes=64) for c in range(TILES)]
+        w_bf, w_codes, w_sc = {}, {}, {}
 
-        def round_w1(c, a):
-            nc.scalar.copy(
-                w_bf[c][:, a, :, :].rearrange("p (g i) t -> p g t i", i=2),
-                raw[(c, a)][:].rearrange("p t (g i) -> p g t i", i=2),
-            )
-
-        def quantise_w1(c, a0, a1):
-            nc.vector.quantize_mx(
-                out=w_codes[c][:, a0:a1, :].rearrange("p a m -> p (a m)").bitcast(FP8X4),
-                scales=w_sc[c][:, a0:a1, :].rearrange("p a m -> p (a m)"),
-                in_=w_bf[c][:, a0:a1, :, :].rearrange("p a m t -> p (a m t)"),
-            )
-
-        h = {}
-
-        def energy(c):
-            banks = [psum.tile([P, BANK], F32, name="acc", tag="bank%d" % (2 * (c % 3) + b)) for b in range(HALVES)]
-            order = [(a, b) for a in range(PASSES) for b in range(HALVES)]
-            if c > 0:
-                order = [(a, b) for b in range(HALVES) for a in range(PASSES)]
-            for a, b in order:
-                nc.tensor.matmul_mx(
-                    out=banks[b][:],
-                    lhsT=w_codes[c][:, a, :].bitcast(FP8X4),
-                    lhsT_scale=w_sc[c][:, a, :],
-                    rhs=v_codes[(a, b)][:].bitcast(FP8X4),
-                    rhs_scale=v_sc[4 * a : P, BANK * b : BANK * (b + 1)],
-                    start=(a == 0),
-                    stop=(a == PASSES - 1),
-                )
-            h[c] = ring.tile([P, S], F32, name="h", tag="h")
-            for b in range(HALVES):
-                nc.scalar.activation(h[c][:, BANK * b : BANK * (b + 1)], banks[b][:], ACT.Square, bias=no_bias[:])
-
-        picked = {}
-
-        def pick(c, which, j0, j1, after=None):
-            tag = "pick%d_%d_%d" % (c, which, j0) if after is None else "raw%d_1" % after
-            picked[(c, which, j0)] = keep.tile([P, (j1 - j0) * P], F32, name="pick", tag=tag, align_bytes=64)
-            entries = (pos1_sb, pos2_sb)[which][:, LIST_COLS * j0 : LIST_COLS * j1]
-            nc.vector.tensor_copy(picked[(c, which, j0)][:], h[c][:].indirect(entries))
-
-        z_t = [keep.tile([P, GROUPS, 2, 2 * P], BF16, name="zt%d" % a, align_bytes=64) for a in range(PASSES)]
-
-        def amplitude(c, j0, j1, bank_no):
-            bank = psum.tile([P, j1 - j0, 2, P // 2], F32, name="sums", tag="bank%d" % bank_no)
-            for j in range(j1 - j0):
-                for which in range(2):
-                    nc.tensor.matmul(
-                        bank[:, j, :, :].rearrange("p u m -> p (u m)"),
-                        lhsT=picked[(c, which, j0)][:, j * P : (j + 1) * P],
-                        rhs=perm[:],
-                        start=(which == 0),
-                        stop=(which == 1),
-                        is_transpose=True,
-                    )
-            a, place = divmod(c, TILES_PER_PASS)
-            nc.scalar.activation(z_t[a][:, j0:j1, :, P // 2 * place : P // 2 * (place + 1)], bank[:], ACT.Sqrt)
-
-        z_bf = [keep.tile([P, PAIRS, PACK], BF16, name="zbf%d" % a, align_bytes=64) for a in range(PASSES)]
-        z_codes = keep.tile([P, PASSES * PAIRS], U32, name="z_codes", align_bytes=64)
-        z_sc = keep.tile([P, PASSES * PAIRS], U8, name="z_sc", align_bytes=64)
-
-        def z_col(a, j):
-            if a == 0:
-                return EARLY + P * j
-            return P * j if j < GROUPS - 1 else EARLY + PAIRS
-
-        def turn_back(a, j0, j1, bank_no, copy):
-            bank = psum.tile([P, j1 - j0, 2, P], F32, name="turn", tag="bank%d" % bank_no)
-            for j in range(j0, j1):
-                for u in range(2):
-                    nc.tensor.transpose(bank[:, j - j0, u, :], z_t[a][:, j, u, :].bitcast(F32), ident[:])
+        def round_w1(a, b, u, copy, m0=0, m1=P):
+            if m0 == 0:
+                w_bf[(a, b, u)] = keep.tile([P, 2, P, PACK], BF16, name="wbf%d_%d_%d" % (a, b, u), align_bytes=64)
             copy(
-                z_bf[a][:, P * j0 : P * j1, :].bitcast(F32).rearrange("p (j n) u -> p j n u", n=P),
-                bank[:].rearrange("p j u n -> p j n u"),
+                w_bf[(a, b, u)][:].rearrange("p e m kk -> p m kk e")[:, m0:m1, :, :],
+                raw[(a, b)][:].rearrange("p kk (m t) -> p m kk t", t=PACK)[:, m0:m1, :, 2 * u : 2 * u + 2],
             )
 
-        def quantise_z(a, j0, j1):
-            at = slice(z_col(a, j0), z_col(a, j0) + P * (j1 - j0))
+        def quantise_w1(a, b, u):
+            w_codes[(a, b, u)] = keep.tile([P, 2 * P], U32, name="wc%d_%d_%d" % (a, b, u), align_bytes=64)
+            w_sc[(a, b, u)] = keep.tile([P, 2 * P], U8, name="ws%d_%d_%d" % (a, b, u), align_bytes=64)
             nc.vector.quantize_mx(
-                out=z_codes[:, at].bitcast(FP8X4),
-                scales=z_sc[:, at],
-                in_=z_bf[a][:, P * j0 : P * j1, :].rearrange("p n t -> p (n t)"),
+                out=w_codes[(a, b, u)][:].bitcast(FP8X4),
+                scales=w_sc[(a, b, u)][:],
+                in_=w_bf[(a, b, u)][:].rearrange("p e m kk -> p (e m kk)"),
             )
 
-        def score_pass(dst, t, a, j, width):
-            at = slice(z_col(a, j), z_col(a, j) + width)
+        acc = {}
+
+        def energy_pass(c, a, half):
+            b, t = divmod(c, PACK)
+            u, e = divmod(t, 2)
+            if a == 0:
+                acc[(c, half)] = psum.tile([P, BANK], F32, name="acc", tag="bank%d" % (2 * t + half))
             nc.tensor.matmul_mx(
-                out=dst,
-                lhsT=w2_sb[:, a, 2 * P * t : 2 * P * (t + 1)].bitcast(FP4X4),
-                lhsT_scale=w2_sc[:, a, :].bitcast(U8)[:, P * t : P * (t + 1)],
-                rhs=z_codes[:, at].bitcast(FP8X4),
-                rhs_scale=z_sc[:, at],
+                out=acc[(c, half)][:],
+                lhsT=w_codes[(a, b, u)][:, P * e : P * (e + 1)].bitcast(FP8X4),
+                lhsT_scale=w_sc[(a, b, u)][:, P * e : P * (e + 1)],
+                rhs=v_codes[(a, half)][:].bitcast(FP8X4),
+                rhs_scale=v_sc[4 * a : P, BANK * half : BANK * (half + 1)],
                 start=(a == 0),
                 stop=(a == PASSES - 1),
             )
 
-        gather_tab(0, 0)
-        round_w1(0, 0)
-        gather_tab(0, 1)
-        nc.vector.tensor_copy(v_sc[:], tab_sc[:].bitcast(U8).indirect(offs_sb[:]))
-        quantise_w1(0, 0, 1)
-        gather_tab(1, 0)
-        round_w1(0, 1)
-        quantise_w1(0, 1, 2)
-        gather_tab(1, 1)
-        energy(0)
+        h = {}
 
-        for a in range(PASSES):
-            round_w1(1, a)
-        quantise_w1(1, 0, PASSES)
-        for a in range(PASSES):
-            round_w1(2, a)
-        energy(1)
-        pick(0, 0, 0, GROUPS, after=1)
-        quantise_w1(2, 0, PASSES)
-        pick(0, 1, 0, GROUPS, after=2)
-        for a in range(PASSES):
-            round_w1(3, a)
+        def square(c):
+            h[c] = keep.tile([P, S], F32, name="h%d" % c, align_bytes=64)
+            for half in range(HALVES):
+                nc.scalar.activation(h[c][:, BANK * half : BANK * (half + 1)], acc[(c, half)][:], ACT.Square, bias=no_bias[:])
 
-        last = TILES - 1
-        for c in range(1, last - 1):
-            quantise_w1(c + 2, 0, PASSES)
-            energy(c + 1)
-            if c + 3 <= last:
+        sums = [keep.tile([P, PACK, PAIRS], F32, name="sums%d" % b, align_bytes=64) for b in range(PASSES)]
+        first = {}
+
+        def pick_first(c, j0, width, tag=None):
+            first[(c, j0)] = keep.tile([P, width], F32, name="first", tag=tag or "first%d_%d" % (c, j0), align_bytes=64)
+            nc.vector.tensor_copy(first[(c, j0)][:], h[c][:].indirect(pos1_sb[:, j0 // 16 : (j0 + width) // 16]))
+
+        def pick_add(c, j0, width):
+            b, t = divmod(c, PACK)
+            nc.vector.tensor_tensor(
+                sums[b][:, t, j0 : j0 + width],
+                h[c][:].indirect(pos2_sb[:, j0 // 16 : (j0 + width) // 16]),
+                first[(c, j0)][:],
+                ADD,
+            )
+
+        def pick(c, width):
+            starts = list(range(0, PAIRS, width))
+            pick_first(c, starts[0], width)
+            for i, j0 in enumerate(starts):
+                if i + 1 < len(starts):
+                    pick_first(c, starts[i + 1], width)
+                pick_add(c, j0, width)
+
+        z_bf, z_codes, z_sc = {}, {}, {}
+
+        def root(b, j0, width):
+            z_bf[(b, j0)] = keep.tile([P, width, PACK], BF16, name="zbf%d_%d" % (b, j0), align_bytes=64)
+            nc.scalar.activation(
+                z_bf[(b, j0)][:].rearrange("p (g i) t -> p g t i", i=4),
+                sums[b][:, :, j0 : j0 + width].rearrange("p t (g i) -> p g t i", i=4),
+                ACT.Sqrt,
+            )
+
+        def quantise_z(b, j0, width):
+            if j0 == 0:
+                z_codes[b] = keep.tile([P, PAIRS], U32, name="zc%d" % b, align_bytes=64)
+                z_sc[b] = keep.tile([P, PAIRS], U8, name="zs%d" % b, align_bytes=64)
+            nc.vector.quantize_mx(
+                out=z_codes[b][:, j0 : j0 + width].bitcast(FP8X4),
+                scales=z_sc[b][:, j0 : j0 + width],
+                in_=z_bf[(b, j0)][:].rearrange("p n t -> p (n t)"),
+            )
+
+        scores = {}
+
+        def score_pass(n, b, j0, width):
+            if b == 0:
+                scores[n] = psum.tile([P, BANK], F32, name="score", tag="bank%d" % n)
+            nc.tensor.matmul_mx(
+                out=scores[n][:, j0 : j0 + width],
+                lhsT=w2_sb[:, b, 2 * P * n : 2 * P * (n + 1)].bitcast(FP4X4),
+                lhsT_scale=w2_sc[:, b, :].bitcast(U8)[:, P * n : P * (n + 1)],
+                rhs=z_codes[b][:, j0 : j0 + width].bitcast(FP8X4),
+                rhs_scale=z_sc[b][:, j0 : j0 + width],
+                start=(b == 0),
+                stop=(b == PASSES - 1 and j0 + width == PAIRS),
+            )
+
+        def energy(c):
+            for half in range(HALVES):
                 for a in range(PASSES):
-                    round_w1(c + 3, a)
-            pick(c, 0, 0, GROUPS, after=c + 2)
-            pick(c, 1, 0, GROUPS)
-            amplitude(c - 1, 0, GROUPS, SUM_BANK[c - 1])
+                    energy_pass(c, a, half)
 
-        for half in range(2):
-            turn_back(0, 2 * half, 2 * half + 2, TURN_BANK[half], nc.scalar.copy)
-        energy(last)
-        pick(last - 1, 0, 0, GROUPS)
-        quantise_z(0, 0, GROUPS)
-        pick(last - 1, 1, 0, GROUPS)
-        amplitude(last - 2, 0, GROUPS, SUM_BANK[last - 2])
-        scores = [psum.tile([P, BANK], F32, name="score", tag="bank%d" % SCORE_BANK[t]) for t in range(CLASS_TILES)]
-        for t in range(CLASS_TILES):
-            score_pass(scores[t][:], t, 0, 0, BANK)
-        amplitude(last - 1, 0, GROUPS, SUM_BANK[last - 1])
+        for u in range(2):
+            round_w1(0, 0, u, nc.scalar.copy)
+        for u in range(2):
+            quantise_w1(0, 0, u)
+        for half in range(HALVES):
+            gather_tab(0, half)
+        nc.vector.tensor_copy(v_sc[:], tab_sc[:].bitcast(U8).indirect(offs_sb[:]))
+        for c in range(2):
+            for half in range(HALVES):
+                energy_pass(c, 0, half)
+        for half in range(HALVES):
+            gather_tab(1, half)
+        round_w1(1, 0, 0, nc.scalar.copy, 0, P // 2)
+        round_w1(1, 0, 0, nc.vector.tensor_copy, P // 2, P)
+        quantise_w1(1, 0, 0)
+        round_w1(1, 0, 1, nc.vector.tensor_copy)
+        quantise_w1(1, 0, 1)
+        for c in range(2):
+            for half in range(HALVES):
+                energy_pass(c, 1, half)
+        energy(2)
+        energy(3)
 
-        for j in range(GROUPS):
-            pick(last, 0, j, j + 1)
-            pick(last, 1, j, j + 1)
-        for j in range(GROUPS):
-            amplitude(last, j, j + 1, LAST_BANK[j])
-            if j > 0:
-                turn_back(1, j - 1, j, LAST_BANK[j - 1], nc.vector.tensor_copy)
-        quantise_z(1, 0, 2)
-        quantise_z(1, 2, GROUPS - 1)
-        turn_back(1, GROUPS - 1, GROUPS, LAST_BANK[GROUPS - 1], nc.vector.tensor_copy)
-        for t in range(CLASS_TILES):
-            score_pass(scores[t][:], t, 1, 0, BANK)
-        quantise_z(1, GROUPS - 1, GROUPS)
-        late = [psum.tile([P, 2, P], F32, name="late", tag="bank%d" % bank_no) for bank_no in LATE_BANK]
-        for t in range(CLASS_TILES):
-            for a in range(PASSES):
-                score_pass(late[t // 2][:, t % 2, :], t, a, GROUPS - 1, P)
+        WIDE = 256
+        square(0)
+        pick(0, WIDE)
+        square(1)
+        pick(1, WIDE)
+        for a in range(PASSES):
+            round_w1(a, 1, 0, nc.scalar.copy)
+        square(2)
+        pick(2, WIDE)
+        for a in range(PASSES):
+            quantise_w1(a, 1, 0)
+        energy(4)
+        energy(5)
+        square(3)
+        pick(3, WIDE)
+        for a in range(PASSES):
+            round_w1(a, 1, 1, nc.scalar.copy)
+        for a in range(PASSES):
+            quantise_w1(a, 1, 1)
+        energy(6)
+        energy(7)
+        square(4)
+        pick(4, WIDE)
+        square(5)
+        pick(5, WIDE)
+        root(0, 0, PAIRS)
+        quantise_z(0, 0, PAIRS)
+        for n in range(CLASS_TILES):
+            score_pass(n, 0, 0, PAIRS)
+        square(6)
+        square(7)
+        for j0 in range(0, PAIRS, P):
+            pick_first(6, j0, P, "first7_%d" % (j0 - 2 * P) if j0 >= 2 * P else None)
+            pick_first(7, j0, P)
+            pick_add(6, j0, P)
+            pick_add(7, j0, P)
+        for j0 in range(0, PAIRS, P):
+            root(1, j0, P)
+            quantise_z(1, j0, P)
+        for n in range(CLASS_TILES):
+            score_pass(n, 1, 0, PAIRS)
 
-        for t in range(CLASS_TILES):
-            res = ring.tile([P, EARLY], F32, name="res", tag="res")
-            nc.scalar.activation(res[:], scores[t][:, :EARLY], ACT.Sigmoid, bias=bias[:, t : t + 1])
-            nc.sync.dma_start(out[P * t : P * (t + 1), :EARLY], res[:])
-        for g in range(len(late)):
-            res_late = ring.tile([P, 2, P], F32, name="res_late", tag="res_late")
-            for i in range(2):
-                t = 2 * g + i
-                nc.scalar.activation(res_late[:, i, :], late[g][:, i, :], ACT.Sigmoid, bias=bias[:, t : t + 1])
-            nc.sync.dma_start(out[2 * P * g : 2 * P * (g + 1), EARLY:].rearrange("(t p) n -> p t n", p=P), res_late[:])
+        for n in range(CLASS_TILES):
+            width = PAIRS if n + 1 < CLASS_TILES else PAIRS // 2
+            for j0 in range(0, PAIRS, width):
+                res = keep.tile([P, width], F32, name="res%d_%d" % (n, j0), align_bytes=64)
+                nc.scalar.activation(res[:], scores[n][:, j0 : j0 + width], ACT.Sigmoid, bias=bias[:, n : n + 1])
+                nc.sync.dma_start(out[P * n : P * (n + 1), j0 : j0 + width], res[:])

@@ -30,63 +30,64 @@ def tile_list_seismic_arrival_score_kernel(tc, tab_words, tab_scales, offs, pos1
     nc = tc.nc
     with ExitStack() as ctx:
         keep = ctx.enter_context(tc.tile_pool(name="keep", bufs=1))
+        stage = ctx.enter_context(tc.tile_pool(name="stage", bufs=1))
         psum = ctx.enter_context(tc.psum_pool(name="psum", bufs=1))
 
         offs_sb = keep.tile([P, S // 16], U16, name="offs_sb")
         pos1_sb = keep.tile([P, PAIRS // 16], U16, name="pos1_sb")
         pos2_sb = keep.tile([P, PAIRS // 16], U16, name="pos2_sb")
-        tab_sb = [keep.tile([P, T], I32, name="tab%d" % a, align_bytes=64) for a in range(PASSES)]
+        KB = 1024
+        shared = {
+            "tab0": 4 * KB, "raw0_1": 0, "w2_sb": 8 * KB, "w2_sc": 10 * KB, "bias": 11 * KB, "raw1_1": 16 * KB,
+            "wbf1_0_0": 26 * KB, "wbf1_0_1": 26 * KB,
+            "first6_0": 24 * KB, "first7_256": 24 * KB, "first6_384": 24 * KB,
+            "first7_0": 25 * KB, "first6_256": 25 * KB, "first7_384": 25 * KB,
+        }
+
+        def new_tile(shape, dtype, name):
+            if name in shared:
+                return stage.tile(shape, dtype, name=name, offset=shared[name], align_bytes=64)
+            return keep.tile(shape, dtype, name=name, align_bytes=64)
+
+        tab_sb = [new_tile([P, T], I32, "tab%d" % a) for a in range(PASSES)]
         tab_sc = keep.tile([P, T // 4], I32, name="tab_sc", align_bytes=64)
-        w2_sb = keep.tile([P, PASSES, 2 * N], U8, name="w2_sb", align_bytes=64)
-        w2_sc = keep.tile([P, PASSES, N // 4], I32, name="w2_sc", align_bytes=64)
-        bias = keep.tile([P, CLASS_TILES], F32, name="bias")
         zero = keep.tile([P, 1], F32, name="zero")
         no_bias = keep.tile([P, 1], F32, name="no_bias")
 
         nc.vector.memset(tab_sc[:, : T // 8], 0)
         nc.gpsimd.memset(tab_sc[:, T // 8 :], 0)
-        nc.vector.memset(w2_sc[:], 0)
         nc.vector.memset(zero[:], 0.0)
         nc.scalar.activation(no_bias[:], zero[:], ACT.Sqrt)
 
         raw = {}
 
         def load_w1(a, b):
-            raw[(a, b)] = keep.tile([P, PACK, K_PASS], F32, name="raw%d_%d" % (a, b), align_bytes=64)
+            raw[(a, b)] = new_tile([P, PACK, K_PASS], F32, "raw%d_%d" % (a, b))
             rows = w1[a * K_PASS : (a + 1) * K_PASS, b * K_PASS : (b + 1) * K_PASS]
             nc.sync.dma_start(raw[(a, b)][:], rows.rearrange("(p t) m -> p t m", t=PACK))
 
         def load_tab(a):
             nc.sync.dma_start(tab_sb[a][:], tab_words[a].rearrange("p t i -> p (t i)").bitcast(I32))
 
-        def load_tab_scales(i):
-            s, a = divmod(i, PASSES)
-            nc.sync.dma_start(tab_sc[4 * a + s : P : 32, :], tab_scales[a, s:16:4, :].bitcast(I32))
-
         load_w1(0, 0)
         nc.sync.dma_start(offs_sb[:], offs)
         nc.sync.dma_start(pos1_sb[:], pos1)
         nc.sync.dma_start(pos2_sb[:], pos2)
-        for i in range(2):
-            load_tab_scales(i)
+        for a in range(PASSES):
+            nc.sync.dma_start(tab_sc[4 * a : P : 8, :], tab_scales[a].bitcast(I32))
         load_tab(0)
-        for i in range(2, 8):
-            load_tab_scales(i)
         load_tab(1)
         load_w1(1, 0)
-        load_w1(0, 1)
-        load_w1(1, 1)
-        nc.sync.dma_start(w2_sb[:], w2_words.rearrange("a p n -> p a n"))
-        for q in range(4):
-            nc.sync.dma_start(
-                w2_sc[32 * q : 32 * q + 4, :, :],
-                w2_scales[:, 4 * q : 4 * q + 4, :].bitcast(I32).rearrange("a g n -> g a n"),
-            )
-        with nc.allow_non_contiguous_dma(reason="one bias value a partition"):
-            nc.sync.dma_start(bias[:], b2.rearrange("(t p) -> p t", p=P))
+
+        picked_sc = keep.tile([P, S], U8, name="picked_sc", align_bytes=64)
+        nc.vector.tensor_copy(picked_sc[:], tab_sc[:].bitcast(U8).indirect(offs_sb[:]))
+        v_sc = keep.tile([P, S // 4], I32, name="v_sc", align_bytes=64)
+        nc.vector.tensor_copy(v_sc[:], picked_sc[:].bitcast(I32))
+        for a in range(PASSES):
+            for s in range(1, 4):
+                nc.scalar.dma_start(v_sc[4 * a + s : P : 32, :], picked_sc[4 * a + 8 * s : P : 32, :].bitcast(I32))
 
         v_codes = {}
-        v_sc = keep.tile([P, S], U8, name="v_sc", align_bytes=64)
 
         def gather_tab(a, half):
             v_codes[(a, half)] = keep.tile([P, BANK], U32, name="v%d_%d" % (a, half), align_bytes=64)
@@ -97,7 +98,7 @@ def tile_list_seismic_arrival_score_kernel(tc, tab_words, tab_scales, offs, pos1
 
         def round_w1(a, b, u, copy, m0=0, m1=P):
             if m0 == 0:
-                w_bf[(a, b, u)] = keep.tile([P, 2, P, PACK], BF16, name="wbf%d_%d_%d" % (a, b, u), align_bytes=64)
+                w_bf[(a, b, u)] = new_tile([P, 2, P, PACK], BF16, "wbf%d_%d_%d" % (a, b, u))
             copy(
                 w_bf[(a, b, u)][:].rearrange("p e m kk -> p m kk e")[:, m0:m1, :, :],
                 raw[(a, b)][:].rearrange("p kk (m t) -> p m kk t", t=PACK)[:, m0:m1, :, 2 * u : 2 * u + 2],
@@ -117,16 +118,17 @@ def tile_list_seismic_arrival_score_kernel(tc, tab_words, tab_scales, offs, pos1
         def energy_pass(c, a, half):
             b, t = divmod(c, PACK)
             u, e = divmod(t, 2)
-            if a == 0:
+            opens = a == (1 if 0 < c < PACK else 0)
+            if opens:
                 acc[(c, half)] = psum.tile([P, BANK], F32, name="acc", tag="bank%d" % (2 * t + half))
             nc.tensor.matmul_mx(
                 out=acc[(c, half)][:],
                 lhsT=w_codes[(a, b, u)][:, P * e : P * (e + 1)].bitcast(FP8X4),
                 lhsT_scale=w_sc[(a, b, u)][:, P * e : P * (e + 1)],
                 rhs=v_codes[(a, half)][:].bitcast(FP8X4),
-                rhs_scale=v_sc[4 * a : P, BANK * half : BANK * (half + 1)],
-                start=(a == 0),
-                stop=(a == PASSES - 1),
+                rhs_scale=v_sc[:].bitcast(U8)[4 * a : P, BANK * half : BANK * (half + 1)],
+                start=opens,
+                stop=not opens,
             )
 
         h = {}
@@ -136,11 +138,11 @@ def tile_list_seismic_arrival_score_kernel(tc, tab_words, tab_scales, offs, pos1
             for half in range(HALVES):
                 nc.scalar.activation(h[c][:, BANK * half : BANK * (half + 1)], acc[(c, half)][:], ACT.Square, bias=no_bias[:])
 
-        sums = [keep.tile([P, PACK, PAIRS], F32, name="sums%d" % b, align_bytes=64) for b in range(PASSES)]
+        sums = [new_tile([P, PACK, PAIRS], F32, "sums%d" % b) for b in range(PASSES)]
         first = {}
 
-        def pick_first(c, j0, width, tag=None):
-            first[(c, j0)] = keep.tile([P, width], F32, name="first", tag=tag or "first%d_%d" % (c, j0), align_bytes=64)
+        def pick_first(c, j0, width):
+            first[(c, j0)] = new_tile([P, width], F32, "first%d_%d" % (c, j0))
             nc.vector.tensor_copy(first[(c, j0)][:], h[c][:].indirect(pos1_sb[:, j0 // 16 : (j0 + width) // 16]))
 
         def pick_add(c, j0, width):
@@ -163,7 +165,7 @@ def tile_list_seismic_arrival_score_kernel(tc, tab_words, tab_scales, offs, pos1
         z_bf, z_codes, z_sc = {}, {}, {}
 
         def root(b, j0, width):
-            z_bf[(b, j0)] = keep.tile([P, width, PACK], BF16, name="zbf%d_%d" % (b, j0), align_bytes=64)
+            z_bf[(b, j0)] = new_tile([P, width, PACK], BF16, "zbf%d_%d" % (b, j0))
             nc.scalar.activation(
                 z_bf[(b, j0)][:].rearrange("p (g i) t -> p g t i", i=4),
                 sums[b][:, :, j0 : j0 + width].rearrange("p t (g i) -> p g t i", i=4),
@@ -197,7 +199,7 @@ def tile_list_seismic_arrival_score_kernel(tc, tab_words, tab_scales, offs, pos1
 
         def energy(c):
             for half in range(HALVES):
-                for a in range(PASSES):
+                for a in (1, 0) if c < PACK else (0, 1):
                     energy_pass(c, a, half)
 
         for u in range(2):
@@ -206,10 +208,22 @@ def tile_list_seismic_arrival_score_kernel(tc, tab_words, tab_scales, offs, pos1
             quantise_w1(0, 0, u)
         for half in range(HALVES):
             gather_tab(0, half)
-        nc.vector.tensor_copy(v_sc[:], tab_sc[:].bitcast(U8).indirect(offs_sb[:]))
-        for c in range(2):
-            for half in range(HALVES):
-                energy_pass(c, 0, half)
+        load_w1(0, 1)
+        load_w1(1, 1)
+        w2_sb = new_tile([P, PASSES, 2 * N], U8, "w2_sb")
+        w2_sc = new_tile([P, PASSES, N // 4], I32, "w2_sc")
+        bias = new_tile([P, CLASS_TILES], F32, "bias")
+        nc.vector.memset(w2_sc[:], 0)
+        nc.sync.dma_start(w2_sb[:], w2_words.rearrange("a p n -> p a n"))
+        for q in range(4):
+            nc.sync.dma_start(
+                w2_sc[32 * q : 32 * q + 4, :, :],
+                w2_scales[:, 4 * q : 4 * q + 4, :].bitcast(I32).rearrange("a g n -> g a n"),
+            )
+        with nc.allow_non_contiguous_dma(reason="one bias value a partition"):
+            nc.sync.dma_start(bias[:], b2.rearrange("(t p) -> p t", p=P))
+        for half in range(HALVES):
+            energy_pass(0, 0, half)
         for half in range(HALVES):
             gather_tab(1, half)
         round_w1(1, 0, 0, nc.scalar.copy, 0, P // 2)
@@ -217,9 +231,11 @@ def tile_list_seismic_arrival_score_kernel(tc, tab_words, tab_scales, offs, pos1
         quantise_w1(1, 0, 0)
         round_w1(1, 0, 1, nc.vector.tensor_copy)
         quantise_w1(1, 0, 1)
-        for c in range(2):
-            for half in range(HALVES):
-                energy_pass(c, 1, half)
+        for half in range(HALVES):
+            energy_pass(0, 1, half)
+        for half in range(HALVES):
+            for a in (1, 0):
+                energy_pass(1, a, half)
         energy(2)
         energy(3)
 
@@ -254,14 +270,16 @@ def tile_list_seismic_arrival_score_kernel(tc, tab_words, tab_scales, offs, pos1
             score_pass(n, 0, 0, PAIRS)
         square(6)
         square(7)
-        for j0 in range(0, PAIRS, P):
-            pick_first(6, j0, P, "first7_%d" % (j0 - 2 * P) if j0 >= 2 * P else None)
-            pick_first(7, j0, P)
-            pick_add(6, j0, P)
-            pick_add(7, j0, P)
-        for j0 in range(0, PAIRS, P):
-            root(1, j0, P)
-            quantise_z(1, j0, P)
+        groups = ((0, WIDE), (WIDE, P), (WIDE + P, P))
+        for g, (j0, width) in enumerate(groups):
+            order = (6, 7) if g % 2 == 0 else (7, 6)
+            for c in order:
+                pick_first(c, j0, width)
+            for c in order:
+                pick_add(c, j0, width)
+        for j0, width in groups:
+            root(1, j0, width)
+            quantise_z(1, j0, width)
         for n in range(CLASS_TILES):
             score_pass(n, 1, 0, PAIRS)
 

@@ -167,8 +167,8 @@ def tile_list_seismic_arrival_score_kernel(tc, tab_words, tab_scales, offs, pos1
         def root(b, j0, width):
             z_bf[(b, j0)] = new_tile([P, width, PACK], BF16, "zbf%d_%d" % (b, j0))
             nc.scalar.activation(
-                z_bf[(b, j0)][:].rearrange("p (g i) t -> p g t i", i=4),
-                sums[b][:, :, j0 : j0 + width].rearrange("p t (g i) -> p g t i", i=4),
+                z_bf[(b, j0)][:],
+                sums[b][:, :, j0 : j0 + width].rearrange("p t j -> p j t"),
                 ACT.Sqrt,
             )
 

@@ -39,7 +39,7 @@ def tile_list_seismic_arrival_score_kernel(tc, tab_words, tab_scales, offs, pos1
         KB = 1024
         shared = {
             "tab0": 4 * KB, "raw0_1": 0, "w2_sb": 8 * KB, "w2_sc": 10 * KB, "bias": 11 * KB, "raw1_1": 16 * KB,
-            "wbf1_0_0": 26 * KB, "wbf1_0_1": 26 * KB,
+            "zc0": 22 * KB + 512, "wbf1_0_0": 26 * KB, "wbf1_0_1": 26 * KB,
             "first6_0": 24 * KB, "first7_256": 24 * KB, "first6_384": 24 * KB,
             "first7_0": 25 * KB, "first6_256": 25 * KB, "first7_384": 25 * KB,
         }
@@ -174,7 +174,7 @@ def tile_list_seismic_arrival_score_kernel(tc, tab_words, tab_scales, offs, pos1
 
         def quantise_z(b, j0, width):
             if j0 == 0:
-                z_codes[b] = keep.tile([P, PAIRS], U32, name="zc%d" % b, align_bytes=64)
+                z_codes[b] = new_tile([P, PAIRS], U32, "zc%d" % b)
                 z_sc[b] = keep.tile([P, PAIRS], U8, name="zs%d" % b, align_bytes=64)
             nc.vector.quantize_mx(
                 out=z_codes[b][:, j0 : j0 + width].bitcast(FP8X4),
@@ -265,9 +265,6 @@ def tile_list_seismic_arrival_score_kernel(tc, tab_words, tab_scales, offs, pos1
         square(5)
         pick(5, WIDE)
         root(0, 0, PAIRS)
-        quantise_z(0, 0, PAIRS)
-        for n in range(CLASS_TILES):
-            score_pass(n, 0, 0, PAIRS)
         square(6)
         square(7)
         groups = ((0, WIDE), (WIDE, P), (WIDE + P, P))
@@ -277,11 +274,13 @@ def tile_list_seismic_arrival_score_kernel(tc, tab_words, tab_scales, offs, pos1
                 pick_first(c, j0, width)
             for c in order:
                 pick_add(c, j0, width)
+        quantise_z(0, 0, PAIRS)
         for j0, width in groups:
             root(1, j0, width)
             quantise_z(1, j0, width)
         for n in range(CLASS_TILES):
-            score_pass(n, 1, 0, PAIRS)
+            for b in range(PASSES):
+                score_pass(n, b, 0, PAIRS)
 
         for n in range(CLASS_TILES):
             width = PAIRS if n + 1 < CLASS_TILES else PAIRS // 2

@@ -38,10 +38,11 @@ def tile_list_seismic_arrival_score_kernel(tc, tab_words, tab_scales, offs, pos1
         pos2_sb = keep.tile([P, PAIRS // 16], U16, name="pos2_sb")
         KB = 1024
         shared = {
-            "tab0": 4 * KB, "raw0_1": 0, "w2_sb": 8 * KB, "w2_sc": 10 * KB, "bias": 11 * KB, "raw1_1": 16 * KB,
-            "zc0": 22 * KB + 512, "wbf1_0_0": 26 * KB, "wbf1_0_1": 26 * KB,
-            "first6_0": 24 * KB, "first7_256": 24 * KB, "first6_384": 24 * KB,
-            "first7_0": 25 * KB, "first6_256": 25 * KB, "first7_384": 25 * KB,
+            "tab0": 12 * KB, "raw1_0": 5 * KB, "w2_sb": 13 * KB, "w2_sc": 15 * KB, "bias": 16 * KB,
+            "raw0_1": 17 * KB, "raw1_1": 25 * KB,
+            "zc0": 38 * KB + 512, "wbf1_0_0": 42 * KB, "wbf1_0_1": 42 * KB,
+            "first6_0": 40 * KB, "first7_256": 40 * KB, "first6_384": 40 * KB,
+            "first7_0": 41 * KB, "first6_256": 41 * KB, "first7_384": 41 * KB,
         }
 
         def new_tile(shape, dtype, name):
@@ -66,18 +67,24 @@ def tile_list_seismic_arrival_score_kernel(tc, tab_words, tab_scales, offs, pos1
             rows = w1[a * K_PASS : (a + 1) * K_PASS, b * K_PASS : (b + 1) * K_PASS]
             nc.sync.dma_start(raw[(a, b)][:], rows.rearrange("(p t) m -> p t m", t=PACK))
 
+        def load_row_pair(g):
+            if g == 0:
+                raw[(0, 0)] = new_tile([P, PACK, K_PASS], F32, "raw0_0")
+            rows = w1[:K_PASS, :K_PASS].rearrange("(p t) m -> p t m", t=PACK)
+            nc.sync.dma_start(raw[(0, 0)][:, 2 * g : 2 * g + 2, :], rows[:, 2 * g : 2 * g + 2, :])
+
         def load_tab(a):
             nc.sync.dma_start(tab_sb[a][:], tab_words[a].rearrange("p t i -> p (t i)").bitcast(I32))
 
-        load_w1(0, 0)
+        load_row_pair(0)
         nc.sync.dma_start(offs_sb[:], offs)
         nc.sync.dma_start(pos1_sb[:], pos1)
         nc.sync.dma_start(pos2_sb[:], pos2)
         for a in range(PASSES):
             nc.sync.dma_start(tab_sc[4 * a : P : 8, :], tab_scales[a].bitcast(I32))
         load_tab(0)
+        load_row_pair(1)
         load_tab(1)
-        load_w1(1, 0)
 
         picked_sc = keep.tile([P, S], U8, name="picked_sc", align_bytes=64)
         nc.vector.tensor_copy(picked_sc[:], tab_sc[:].bitcast(U8).indirect(offs_sb[:]))
@@ -85,7 +92,8 @@ def tile_list_seismic_arrival_score_kernel(tc, tab_words, tab_scales, offs, pos1
         nc.vector.tensor_copy(v_sc[:], picked_sc[:].bitcast(I32))
         for a in range(PASSES):
             for s in range(1, 4):
-                nc.scalar.dma_start(v_sc[4 * a + s : P : 32, :], picked_sc[4 * a + 8 * s : P : 32, :].bitcast(I32))
+                queue = nc.gpsimd if (a, s) == (0, 1) else nc.scalar
+                queue.dma_start(v_sc[4 * a + s : P : 32, :], picked_sc[4 * a + 8 * s : P : 32, :].bitcast(I32))
 
         v_codes = {}
 
@@ -208,6 +216,7 @@ def tile_list_seismic_arrival_score_kernel(tc, tab_words, tab_scales, offs, pos1
             quantise_w1(0, 0, u)
         for half in range(HALVES):
             gather_tab(0, half)
+        load_w1(1, 0)
         load_w1(0, 1)
         load_w1(1, 1)
         w2_sb = new_tile([P, PASSES, 2 * N], U8, "w2_sb")

@@ -175,8 +175,8 @@ def tile_list_seismic_arrival_score_kernel(tc, tab_words, tab_scales, offs, pos1
         def root(b, j0, width):
             z_bf[(b, j0)] = new_tile([P, width, PACK], BF16, "zbf%d_%d" % (b, j0))
             nc.scalar.activation(
-                z_bf[(b, j0)][:],
-                sums[b][:, :, j0 : j0 + width].rearrange("p t j -> p j t"),
+                z_bf[(b, j0)][:].rearrange("p (g i) t -> p g t i", i=4),
+                sums[b][:, :, j0 : j0 + width].rearrange("p t (g i) -> p g t i", i=4),
                 ACT.Sqrt,
             )
 
@@ -235,8 +235,8 @@ def tile_list_seismic_arrival_score_kernel(tc, tab_words, tab_scales, offs, pos1
             energy_pass(0, 0, half)
         for half in range(HALVES):
             gather_tab(1, half)
-        round_w1(1, 0, 0, nc.scalar.copy, 0, P // 2)
-        round_w1(1, 0, 0, nc.vector.tensor_copy, P // 2, P)
+        round_w1(1, 0, 0, nc.scalar.copy, 0, 44)
+        round_w1(1, 0, 0, nc.vector.tensor_copy, 44, P)
         quantise_w1(1, 0, 0)
         round_w1(1, 0, 1, nc.vector.tensor_copy)
         quantise_w1(1, 0, 1)

@@ -24,6 +24,8 @@ BANK = 512
 HALVES = S // BANK
 TILES = H // P
 CLASS_TILES = N // P
+WIDE = PAIRS // 2
+LAST = 64
 
 
 def tile_list_seismic_arrival_score_kernel(tc, tab_words, tab_scales, offs, pos1, pos2, w1, w2_words, w2_scales, b2, out):
@@ -38,11 +40,10 @@ def tile_list_seismic_arrival_score_kernel(tc, tab_words, tab_scales, offs, pos1
         pos2_sb = keep.tile([P, PAIRS // 16], U16, name="pos2_sb")
         KB = 1024
         shared = {
-            "tab0": 12 * KB, "raw1_0": 5 * KB, "w2_sb": 13 * KB, "w2_sc": 15 * KB, "bias": 16 * KB,
-            "raw0_1": 17 * KB, "raw1_1": 25 * KB,
-            "zc0": 38 * KB + 512, "wbf1_0_0": 42 * KB, "wbf1_0_1": 42 * KB,
-            "first6_0": 40 * KB, "first7_256": 40 * KB, "first6_384": 40 * KB,
-            "first7_0": 41 * KB, "first6_256": 41 * KB, "first7_384": 41 * KB,
+            "tab0": 12 * KB, "raw1_0": 4 * KB + 64, "w2_sb": 12 * KB + 64, "w2_sc": 14 * KB + 64, "bias": 15 * KB + 64,
+            "raw0_1": 15 * KB + 512, "wbf0_0_0": 23 * KB + 512, "wbf0_0_1": 25 * KB + 512, "raw1_1": 27 * KB + 512,
+            "first6_0": 36 * KB, "zs0_0": 36 * KB, "zs1_0": 36 * KB + 256, "zs0_1": 36 * KB + 512, "wbf1_0_0": 42 * KB, "wbf1_0_1": 42 * KB,
+            "wc1_1_1": 44 * KB, "zbf0_0": 44 * KB,
         }
 
         def new_tile(shape, dtype, name):
@@ -52,13 +53,13 @@ def tile_list_seismic_arrival_score_kernel(tc, tab_words, tab_scales, offs, pos1
 
         tab_sb = [new_tile([P, T], I32, "tab%d" % a) for a in range(PASSES)]
         tab_sc = keep.tile([P, T // 4], I32, name="tab_sc", align_bytes=64)
-        zero = keep.tile([P, 1], F32, name="zero")
-        no_bias = keep.tile([P, 1], F32, name="no_bias")
+        zero = keep.tile([P, TILES], F32, name="zero")
+        sums = keep.tile([P, TILES * PAIRS], F32, name="sums", align_bytes=64)
 
         nc.vector.memset(tab_sc[:, : T // 8], 0)
         nc.gpsimd.memset(tab_sc[:, T // 8 :], 0)
         nc.vector.memset(zero[:], 0.0)
-        nc.scalar.activation(no_bias[:], zero[:], ACT.Sqrt)
+        nc.scalar.activation(sums[:, 0 : TILES * PAIRS : PAIRS], zero[:], ACT.Sqrt)
 
         raw = {}
 
@@ -97,10 +98,9 @@ def tile_list_seismic_arrival_score_kernel(tc, tab_words, tab_scales, offs, pos1
 
         v_codes = {}
 
-        def gather_tab(a, half):
-            v_codes[(a, half)] = keep.tile([P, BANK], U32, name="v%d_%d" % (a, half), align_bytes=64)
-            entries = offs_sb[:, BANK // 16 * half : BANK // 16 * (half + 1)]
-            nc.vector.tensor_copy(v_codes[(a, half)][:], tab_sb[a][:].bitcast(U32).indirect(entries))
+        def gather_tab(a):
+            v_codes[a] = keep.tile([P, S], U32, name="v%d" % a, align_bytes=64)
+            nc.vector.tensor_copy(v_codes[a][:], tab_sb[a][:].bitcast(U32).indirect(offs_sb[:]))
 
         w_bf, w_codes, w_sc = {}, {}, {}
 
@@ -112,13 +112,14 @@ def tile_list_seismic_arrival_score_kernel(tc, tab_words, tab_scales, offs, pos1
                 raw[(a, b)][:].rearrange("p kk (m t) -> p m kk t", t=PACK)[:, m0:m1, :, 2 * u : 2 * u + 2],
             )
 
-        def quantise_w1(a, b, u):
-            w_codes[(a, b, u)] = keep.tile([P, 2 * P], U32, name="wc%d_%d_%d" % (a, b, u), align_bytes=64)
-            w_sc[(a, b, u)] = keep.tile([P, 2 * P], U8, name="ws%d_%d_%d" % (a, b, u), align_bytes=64)
+        def quantise_w1(a, b, u, e0=0, e1=2):
+            if e0 == 0:
+                w_codes[(a, b, u)] = new_tile([P, 2 * P], U32, "wc%d_%d_%d" % (a, b, u))
+                w_sc[(a, b, u)] = keep.tile([P, 2 * P], U8, name="ws%d_%d_%d" % (a, b, u), align_bytes=64)
             nc.vector.quantize_mx(
-                out=w_codes[(a, b, u)][:].bitcast(FP8X4),
-                scales=w_sc[(a, b, u)][:],
-                in_=w_bf[(a, b, u)][:].rearrange("p e m kk -> p (e m kk)"),
+                out=w_codes[(a, b, u)][:, P * e0 : P * e1].bitcast(FP8X4),
+                scales=w_sc[(a, b, u)][:, P * e0 : P * e1],
+                in_=w_bf[(a, b, u)][:, e0:e1].rearrange("p e m kk -> p (e m kk)"),
             )
 
         acc = {}
@@ -126,14 +127,14 @@ def tile_list_seismic_arrival_score_kernel(tc, tab_words, tab_scales, offs, pos1
         def energy_pass(c, a, half):
             b, t = divmod(c, PACK)
             u, e = divmod(t, 2)
-            opens = a == (1 if 0 < c < PACK else 0)
+            opens = a == 0
             if opens:
                 acc[(c, half)] = psum.tile([P, BANK], F32, name="acc", tag="bank%d" % (2 * t + half))
             nc.tensor.matmul_mx(
                 out=acc[(c, half)][:],
                 lhsT=w_codes[(a, b, u)][:, P * e : P * (e + 1)].bitcast(FP8X4),
                 lhsT_scale=w_sc[(a, b, u)][:, P * e : P * (e + 1)],
-                rhs=v_codes[(a, half)][:].bitcast(FP8X4),
+                rhs=v_codes[a][:, BANK * half : BANK * (half + 1)].bitcast(FP8X4),
                 rhs_scale=v_sc[:].bitcast(U8)[4 * a : P, BANK * half : BANK * (half + 1)],
                 start=opens,
                 stop=not opens,
@@ -143,32 +144,26 @@ def tile_list_seismic_arrival_score_kernel(tc, tab_words, tab_scales, offs, pos1
 
         def square(c):
             h[c] = keep.tile([P, S], F32, name="h%d" % c, align_bytes=64)
+            slot = PAIRS * ((c - 1) % TILES)
             for half in range(HALVES):
-                nc.scalar.activation(h[c][:, BANK * half : BANK * (half + 1)], acc[(c, half)][:], ACT.Square, bias=no_bias[:])
+                nc.scalar.activation(h[c][:, BANK * half : BANK * (half + 1)], acc[(c, half)][:], ACT.Square, bias=sums[:, slot : slot + 1])
 
-        sums = [new_tile([P, PACK, PAIRS], F32, "sums%d" % b) for b in range(PASSES)]
         first = {}
 
         def pick_first(c, j0, width):
-            first[(c, j0)] = new_tile([P, width], F32, "first%d_%d" % (c, j0))
-            nc.vector.tensor_copy(first[(c, j0)][:], h[c][:].indirect(pos1_sb[:, j0 // 16 : (j0 + width) // 16]))
+            if (c, j0) == (TILES - 1, 0):
+                first[(c, j0)] = sums[:, PAIRS * c - width : PAIRS * c]
+            else:
+                first[(c, j0)] = new_tile([P, width], F32, "first%d_%d" % (c, j0))[:]
+            nc.vector.tensor_copy(first[(c, j0)], h[c][:].indirect(pos1_sb[:, j0 // 16 : (j0 + width) // 16]))
 
-        def pick_add(c, j0, width):
-            b, t = divmod(c, PACK)
+        def pick_add(c, j0, width, f0):
             nc.vector.tensor_tensor(
-                sums[b][:, t, j0 : j0 + width],
+                sums[:, PAIRS * c + j0 : PAIRS * c + j0 + width],
                 h[c][:].indirect(pos2_sb[:, j0 // 16 : (j0 + width) // 16]),
-                first[(c, j0)][:],
+                first[(c, f0)][:, j0 - f0 : j0 - f0 + width],
                 ADD,
             )
-
-        def pick(c, width):
-            starts = list(range(0, PAIRS, width))
-            pick_first(c, starts[0], width)
-            for i, j0 in enumerate(starts):
-                if i + 1 < len(starts):
-                    pick_first(c, starts[i + 1], width)
-                pick_add(c, j0, width)
 
         z_bf, z_codes, z_sc = {}, {}, {}
 
@@ -176,46 +171,60 @@ def tile_list_seismic_arrival_score_kernel(tc, tab_words, tab_scales, offs, pos1
             z_bf[(b, j0)] = new_tile([P, width, PACK], BF16, "zbf%d_%d" % (b, j0))
             nc.scalar.activation(
                 z_bf[(b, j0)][:].rearrange("p (g i) t -> p g t i", i=4),
-                sums[b][:, :, j0 : j0 + width].rearrange("p t (g i) -> p g t i", i=4),
+                sums[:].rearrange("p (c j) -> p c j", j=PAIRS)[:, PACK * b : PACK * (b + 1), j0 : j0 + width].rearrange("p t (g i) -> p g t i", i=4),
                 ACT.Sqrt,
             )
 
-        def quantise_z(b, j0, width):
-            if j0 == 0:
-                z_codes[b] = new_tile([P, PAIRS], U32, "zc%d" % b)
-                z_sc[b] = keep.tile([P, PAIRS], U8, name="zs%d" % b, align_bytes=64)
+        z_rows = keep.tile([P, PACK, WIDE], BF16, name="z_rows", align_bytes=64)
+
+        def root_row(c, j0=WIDE, j1=PAIRS):
+            nc.scalar.activation(z_rows[:, c - PACK, j0 - WIDE : j1 - WIDE], sums[:, PAIRS * c + j0 : PAIRS * c + j1], ACT.Sqrt)
+
+        def weave():
+            z_bf[(1, WIDE)] = new_tile([P, WIDE, PACK], BF16, "zbf1_%d" % WIDE)
+            nc.vector.tensor_copy(
+                z_bf[(1, WIDE)][:].rearrange("p (g i) t -> p g t i", i=4),
+                z_rows[:].rearrange("p t (g i) -> p g t i", i=4),
+            )
+
+        def quantise_z(b, j0, width, r0):
+            side, j = divmod(j0, WIDE)
+            if j == 0:
+                z_codes[(b, side)] = new_tile([P, WIDE], U32, "zc%d_%d" % (b, side))
+                z_sc[(b, side)] = new_tile([P, WIDE], U8, "zs%d_%d" % (b, side))
             nc.vector.quantize_mx(
-                out=z_codes[b][:, j0 : j0 + width].bitcast(FP8X4),
-                scales=z_sc[b][:, j0 : j0 + width],
-                in_=z_bf[(b, j0)][:].rearrange("p n t -> p (n t)"),
+                out=z_codes[(b, side)][:, j : j + width].bitcast(FP8X4),
+                scales=z_sc[(b, side)][:, j : j + width],
+                in_=z_bf[(b, r0)][:, j0 - r0 : j0 - r0 + width, :].rearrange("p n t -> p (n t)"),
             )
 
         scores = {}
 
-        def score_pass(n, b, j0, width):
-            if b == 0:
-                scores[n] = psum.tile([P, BANK], F32, name="score", tag="bank%d" % n)
+        def score_pass(n, side, b):
+            opens = b == side
+            if opens:
+                scores[(n, side)] = psum.tile([P, BANK], F32, name="score", tag="bank%d" % (CLASS_TILES * side + n))
             nc.tensor.matmul_mx(
-                out=scores[n][:, j0 : j0 + width],
+                out=scores[(n, side)][:, :WIDE],
                 lhsT=w2_sb[:, b, 2 * P * n : 2 * P * (n + 1)].bitcast(FP4X4),
                 lhsT_scale=w2_sc[:, b, :].bitcast(U8)[:, P * n : P * (n + 1)],
-                rhs=z_codes[b][:, j0 : j0 + width].bitcast(FP8X4),
-                rhs_scale=z_sc[b][:, j0 : j0 + width],
-                start=(b == 0),
-                stop=(b == PASSES - 1 and j0 + width == PAIRS),
+                rhs=z_codes[(b, side)][:].bitcast(FP8X4),
+                rhs_scale=z_sc[(b, side)][:],
+                start=opens,
+                stop=not opens,
             )
 
         def energy(c):
             for half in range(HALVES):
-                for a in (1, 0) if c < PACK else (0, 1):
+                for a in range(PASSES):
                     energy_pass(c, a, half)
 
-        for u in range(2):
-            round_w1(0, 0, u, nc.scalar.copy)
+        gather_tab(0)
+        round_w1(0, 0, 0, nc.scalar.copy)
+        round_w1(0, 0, 1, nc.vector.tensor_copy, 0, P // 2)
+        round_w1(0, 0, 1, nc.scalar.copy, P // 2, P)
         for u in range(2):
             quantise_w1(0, 0, u)
-        for half in range(HALVES):
-            gather_tab(0, half)
         load_w1(1, 0)
         load_w1(0, 1)
         load_w1(1, 1)
@@ -231,69 +240,60 @@ def tile_list_seismic_arrival_score_kernel(tc, tab_words, tab_scales, offs, pos1
             )
         with nc.allow_non_contiguous_dma(reason="one bias value a partition"):
             nc.sync.dma_start(bias[:], b2.rearrange("(t p) -> p t", p=P))
-        for half in range(HALVES):
-            energy_pass(0, 0, half)
-        for half in range(HALVES):
-            gather_tab(1, half)
+        for c in range(PACK):
+            for half in range(HALVES):
+                energy_pass(c, 0, half)
+        gather_tab(1)
         round_w1(1, 0, 0, nc.scalar.copy, 0, 44)
         round_w1(1, 0, 0, nc.vector.tensor_copy, 44, P)
-        quantise_w1(1, 0, 0)
+        quantise_w1(1, 0, 0, 0, 1)
+        quantise_w1(1, 0, 0, 1, 2)
         round_w1(1, 0, 1, nc.vector.tensor_copy)
         quantise_w1(1, 0, 1)
-        for half in range(HALVES):
-            energy_pass(0, 1, half)
-        for half in range(HALVES):
-            for a in (1, 0):
-                energy_pass(1, a, half)
-        energy(2)
-        energy(3)
+        for c in range(PACK):
+            for half in range(HALVES):
+                energy_pass(c, 1, half)
 
-        WIDE = 256
         square(0)
-        pick(0, WIDE)
-        square(1)
-        pick(1, WIDE)
-        for a in range(PASSES):
-            round_w1(a, 1, 0, nc.scalar.copy)
-        square(2)
-        pick(2, WIDE)
-        for a in range(PASSES):
-            quantise_w1(a, 1, 0)
-        energy(4)
-        energy(5)
-        square(3)
-        pick(3, WIDE)
-        for a in range(PASSES):
-            round_w1(a, 1, 1, nc.scalar.copy)
-        for a in range(PASSES):
-            quantise_w1(a, 1, 1)
-        energy(6)
-        energy(7)
-        square(4)
-        pick(4, WIDE)
-        square(5)
-        pick(5, WIDE)
+        pick_first(0, 0, PAIRS)
+        for c in range(1, TILES - 1):
+            square(c)
+            pick_first(c, 0, PAIRS)
+            pick_add(c - 1, 0, PAIRS, 0)
+            if c <= PACK:
+                u, a = divmod(c - 1, 2)
+                round_w1(a, 1, u, nc.scalar.copy)
+                quantise_w1(a, 1, u)
+                if a == 1:
+                    energy(PACK + 2 * u)
+                    energy(PACK + 2 * u + 1)
+        square(TILES - 1)
         root(0, 0, PAIRS)
-        square(6)
-        square(7)
-        groups = ((0, WIDE), (WIDE, P), (WIDE + P, P))
-        for g, (j0, width) in enumerate(groups):
-            order = (6, 7) if g % 2 == 0 else (7, 6)
-            for c in order:
-                pick_first(c, j0, width)
-            for c in order:
-                pick_add(c, j0, width)
-        quantise_z(0, 0, PAIRS)
-        for j0, width in groups:
-            root(1, j0, width)
-            quantise_z(1, j0, width)
-        for n in range(CLASS_TILES):
-            for b in range(PASSES):
-                score_pass(n, b, 0, PAIRS)
-
-        for n in range(CLASS_TILES):
-            width = PAIRS if n + 1 < CLASS_TILES else PAIRS // 2
-            for j0 in range(0, PAIRS, width):
-                res = keep.tile([P, width], F32, name="res%d_%d" % (n, j0), align_bytes=64)
-                nc.scalar.activation(res[:], scores[n][:, j0 : j0 + width], ACT.Sigmoid, bias=bias[:, n : n + 1])
-                nc.sync.dma_start(out[P * n : P * (n + 1), j0 : j0 + width], res[:])
+        for c in range(PACK, TILES - 2):
+            root_row(c)
+        for side in range(2):
+            pick_first(TILES - 1, WIDE * side, WIDE)
+            pick_add(TILES - 2, WIDE * side, WIDE, 0)
+            if side == 0:
+                pick_add(TILES - 1, 0, WIDE, 0)
+        pick_add(TILES - 1, WIDE, WIDE - LAST, WIDE)
+        pick_add(TILES - 1, PAIRS - LAST, LAST, WIDE)
+        root(1, 0, WIDE)
+        root_row(TILES - 2)
+        root_row(TILES - 1, WIDE, PAIRS - LAST)
+        root_row(TILES - 1, PAIRS - LAST, PAIRS)
+        quantise_z(0, 0, WIDE, 0)
+        quantise_z(1, 0, WIDE, 0)
+        quantise_z(0, WIDE, WIDE, 0)
+        weave()
+        quantise_z(1, WIDE, WIDE, WIDE)
+        res = {}
+        for side in range(2):
+            for n in range(CLASS_TILES):
+                for b in (side, 1 - side):
+                    score_pass(n, side, b)
+        for side in range(2):
+            for n in range(CLASS_TILES):
+                res[(n, side)] = keep.tile([P, WIDE], F32, name="res%d_%d" % (n, side), align_bytes=64)
+                nc.scalar.activation(res[(n, side)][:], scores[(n, side)][:, :WIDE], ACT.Sigmoid, bias=bias[:, n : n + 1])
+                nc.sync.dma_start(out[P * n : P * (n + 1), WIDE * side : WIDE * (side + 1)], res[(n, side)][:])

@@ -26,6 +26,8 @@ TILES = H // P
 CLASS_TILES = N // P
 WIDE = PAIRS // 2
 LAST = 64
+NARROW = 256
+CUT = 768
 
 
 def tile_list_seismic_arrival_score_kernel(tc, tab_words, tab_scales, offs, pos1, pos2, w1, w2_words, w2_scales, b2, out):
@@ -40,10 +42,11 @@ def tile_list_seismic_arrival_score_kernel(tc, tab_words, tab_scales, offs, pos1
         pos2_sb = keep.tile([P, PAIRS // 16], U16, name="pos2_sb")
         KB = 1024
         shared = {
-            "tab0": 12 * KB, "raw1_0": 4 * KB + 64, "w2_sb": 12 * KB + 64, "w2_sc": 14 * KB + 64, "bias": 15 * KB + 64,
-            "raw0_1": 15 * KB + 512, "wbf0_0_0": 23 * KB + 512, "wbf0_0_1": 25 * KB + 512, "raw1_1": 27 * KB + 512,
-            "first6_0": 36 * KB, "zs0_0": 36 * KB, "zs1_0": 36 * KB + 256, "zs0_1": 36 * KB + 512, "wbf1_0_0": 42 * KB, "wbf1_0_1": 42 * KB,
-            "wc1_1_1": 44 * KB, "zbf0_0": 44 * KB,
+            "tab0": 12 * KB, "raw0_1": 4 * KB + 64, "dealt": 48 * KB, "z_rows": 48 * KB, "zbf1_0": 50 * KB,
+            "lead": 42 * KB, "v1_768": 42 * KB, "one": 40 * KB, "wbf1_0_1": 40 * KB, "second": 38 * KB, "wbf0_1_1": 38 * KB, "wbf1_1_1": 38 * KB, "narrow1_0": 12 * KB + 64, "narrow0_1": 16 * KB + 64, "narrow1_1": 20 * KB + 64,
+            "w2_sc": 26 * KB + 64, "raw1_1": 27 * KB + 64, "w2_sb": 12 * KB + 64, "bias": 14 * KB + 64,
+            "first6_0": 36 * KB, "zs0_0": 36 * KB, "zs1_0": 36 * KB + 256, "zs0_1": 36 * KB + 512,
+            "wc1_1_1": 46 * KB - 512, "zbf0_0": 44 * KB, "zbf0_256": 46 * KB,
         }
 
         def new_tile(shape, dtype, name):
@@ -59,6 +62,16 @@ def tile_list_seismic_arrival_score_kernel(tc, tab_words, tab_scales, offs, pos1
         nc.vector.memset(tab_sc[:, : T // 8], 0)
         nc.gpsimd.memset(tab_sc[:, T // 8 :], 0)
         nc.vector.memset(zero[:], 0.0)
+        h = [keep.tile([P, S], F32, name="h%d" % c, align_bytes=64) for c in range(TILES)]
+        for c in range(2, 2 + PACK):
+            nc.vector.memset(h[c][:, S - 1 :], 1.0)
+        nc.vector.memset(h[3][:, 0:1], 1.0)
+        one = new_tile([P, 1], F32, "one")
+        nc.vector.memset(one[:], 1.0)
+        lead = new_tile([P, 1], F32, "lead")
+        nc.vector.memset(lead[:], 0.0)
+        second = new_tile([P, 1], F32, "second")
+        nc.vector.memset(second[:], 0.0)
         nc.scalar.activation(sums[:, 0 : TILES * PAIRS : PAIRS], zero[:], ACT.Sqrt)
 
         raw = {}
@@ -68,48 +81,55 @@ def tile_list_seismic_arrival_score_kernel(tc, tab_words, tab_scales, offs, pos1
             rows = w1[a * K_PASS : (a + 1) * K_PASS, b * K_PASS : (b + 1) * K_PASS]
             nc.sync.dma_start(raw[(a, b)][:], rows.rearrange("(p t) m -> p t m", t=PACK))
 
-        def load_row_pair(g):
-            if g == 0:
-                raw[(0, 0)] = new_tile([P, PACK, K_PASS], F32, "raw0_0")
-            rows = w1[:K_PASS, :K_PASS].rearrange("(p t) m -> p t m", t=PACK)
-            nc.sync.dma_start(raw[(0, 0)][:, 2 * g : 2 * g + 2, :], rows[:, 2 * g : 2 * g + 2, :])
+        narrow = {}
 
-        def load_tab(a):
-            nc.sync.dma_start(tab_sb[a][:], tab_words[a].rearrange("p t i -> p (t i)").bitcast(I32))
+        def load_narrow(a, g):
+            narrow[(a, g)] = new_tile([P, PACK, NARROW], F32, "narrow%d_%d" % (a, g))
+            rows = w1[a * K_PASS : (a + 1) * K_PASS, g * NARROW : (g + 1) * NARROW]
+            nc.sync.dma_start(narrow[(a, g)][:], rows.rearrange("(p t) m -> p t m", t=PACK))
 
-        load_row_pair(0)
+        def load_tab(a, t0, t1):
+            nc.sync.dma_start(tab_sb[a][:, t0:t1], tab_words[a].rearrange("p t i -> p (t i)").bitcast(I32)[:, t0:t1])
+
+        load_tab(0, 0, T // 4)
         nc.sync.dma_start(offs_sb[:], offs)
         nc.sync.dma_start(pos1_sb[:], pos1)
         nc.sync.dma_start(pos2_sb[:], pos2)
-        for a in range(PASSES):
-            nc.sync.dma_start(tab_sc[4 * a : P : 8, :], tab_scales[a].bitcast(I32))
-        load_tab(0)
-        load_row_pair(1)
-        load_tab(1)
+        nc.sync.dma_start(tab_sc[0:P:4, :], tab_scales.bitcast(I32).rearrange("a q t -> q a t"))
+        load_tab(0, T // 4, T)
+        load_tab(1, 0, T // 2)
+        load_narrow(0, 0)
+        load_tab(1, T // 2, T)
 
         picked_sc = keep.tile([P, S], U8, name="picked_sc", align_bytes=64)
         nc.vector.tensor_copy(picked_sc[:], tab_sc[:].bitcast(U8).indirect(offs_sb[:]))
-        v_sc = keep.tile([P, S // 4], I32, name="v_sc", align_bytes=64)
-        nc.vector.tensor_copy(v_sc[:], picked_sc[:].bitcast(I32))
+        v_sc = [keep.tile([P, S // 4], I32, name="v_sc%d" % a, align_bytes=64) for a in range(PASSES)]
         for a in range(PASSES):
+            nc.vector.tensor_copy(v_sc[a][:], picked_sc[:].bitcast(I32))
             for s in range(1, 4):
-                queue = nc.gpsimd if (a, s) == (0, 1) else nc.scalar
-                queue.dma_start(v_sc[4 * a + s : P : 32, :], picked_sc[4 * a + 8 * s : P : 32, :].bitcast(I32))
+                queue = nc.gpsimd if a == 1 else nc.scalar
+                queue.dma_start(v_sc[a][4 * a + s : P : 32, :], picked_sc[4 * a + 8 * s : P : 32, :].bitcast(I32))
 
         v_codes = {}
 
-        def gather_tab(a):
-            v_codes[a] = keep.tile([P, S], U32, name="v%d" % a, align_bytes=64)
-            nc.vector.tensor_copy(v_codes[a][:], tab_sb[a][:].bitcast(U32).indirect(offs_sb[:]))
+        def gather_tab(a, i0, i1):
+            v_codes[(a, i0)] = new_tile([P, i1 - i0], U32, "v%d_%d" % (a, i0))
+            nc.vector.tensor_copy(v_codes[(a, i0)][:], tab_sb[a][:].bitcast(U32).indirect(offs_sb[:, i0 // 16 : i1 // 16]))
 
         w_bf, w_codes, w_sc = {}, {}, {}
 
         def round_w1(a, b, u, copy, m0=0, m1=P):
             if m0 == 0:
-                w_bf[(a, b, u)] = new_tile([P, 2, P, PACK], BF16, "wbf%d_%d_%d" % (a, b, u))
+                w_bf[(a, b, u)] = new_tile([P, 2, P, PACK], BF16, "wbf%d_%d_%d" % (a, b, u))[:]
             copy(
-                w_bf[(a, b, u)][:].rearrange("p e m kk -> p m kk e")[:, m0:m1, :, :],
+                w_bf[(a, b, u)].rearrange("p e m kk -> p m kk e")[:, m0:m1, :, :],
                 raw[(a, b)][:].rearrange("p kk (m t) -> p m kk t", t=PACK)[:, m0:m1, :, 2 * u : 2 * u + 2],
+            )
+
+        def round_narrow(a, g, copy, m0=0, m1=P // 2, places=slice(0, 2)):
+            copy(
+                w_bf[(a, 0, g)].rearrange("p e (m s) kk -> p m kk e s", s=2)[:, m0:m1, :, places],
+                narrow[(a, g)][:].rearrange("p kk (m e s) -> p m kk e s", e=2, s=2)[:, m0:m1, :, places],
             )
 
         def quantise_w1(a, b, u, e0=0, e1=2):
@@ -130,23 +150,24 @@ def tile_list_seismic_arrival_score_kernel(tc, tab_words, tab_scales, offs, pos1
             opens = a == 0
             if opens:
                 acc[(c, half)] = psum.tile([P, BANK], F32, name="acc", tag="bank%d" % (2 * t + half))
-            nc.tensor.matmul_mx(
-                out=acc[(c, half)][:],
-                lhsT=w_codes[(a, b, u)][:, P * e : P * (e + 1)].bitcast(FP8X4),
-                lhsT_scale=w_sc[(a, b, u)][:, P * e : P * (e + 1)],
-                rhs=v_codes[a][:, BANK * half : BANK * (half + 1)].bitcast(FP8X4),
-                rhs_scale=v_sc[:].bitcast(U8)[4 * a : P, BANK * half : BANK * (half + 1)],
-                start=opens,
-                stop=not opens,
-            )
-
-        h = {}
+            width = BANK // 2 if (a, half) == (1, 1) else BANK
+            for i0 in range(BANK * half, BANK * (half + 1), width):
+                piece = CUT if a == 1 and i0 >= CUT else 0
+                nc.tensor.matmul_mx(
+                    out=acc[(c, half)][:, i0 - BANK * half : i0 - BANK * half + width],
+                    lhsT=w_codes[(a, b, u)][:, P * e : P * (e + 1)].bitcast(FP8X4),
+                    lhsT_scale=w_sc[(a, b, u)][:, P * e : P * (e + 1)],
+                    rhs=v_codes[(a, piece)][:, i0 - piece : i0 - piece + width].bitcast(FP8X4),
+                    rhs_scale=v_sc[a][:].bitcast(U8)[4 * a : P, i0 : i0 + width],
+                    start=opens,
+                    stop=not opens and i0 + width == BANK * (half + 1),
+                )
 
         def square(c):
-            h[c] = keep.tile([P, S], F32, name="h%d" % c, align_bytes=64)
-            slot = PAIRS * ((c - 1) % TILES)
+            slot = PAIRS * (TILES - 1 if c <= PACK + 1 else c - 1)
             for half in range(HALVES):
-                nc.scalar.activation(h[c][:, BANK * half : BANK * (half + 1)], acc[(c, half)][:], ACT.Square, bias=sums[:, slot : slot + 1])
+                scale = {(1, 0): one[:], (2, 1): h[3][:, 0:1]}.get((c, half), 1.0)
+                nc.scalar.activation(h[c][:, BANK * half : BANK * (half + 1)], acc[(c, half)][:], ACT.Square, bias=sums[:, slot : slot + 1], scale=scale)
 
         first = {}
 
@@ -165,17 +186,28 @@ def tile_list_seismic_arrival_score_kernel(tc, tab_words, tab_scales, offs, pos1
                 ADD,
             )
 
+        dealt = new_tile([P, PACK * PAIRS], F32, "dealt")
+
+        def deal(c):
+            g, e = divmod(c, 2)
+            width = WIDE if c == PACK - 1 else PAIRS
+            for j0 in range(0, PAIRS, width):
+                nc.sync.dma_start(
+                    dealt[64 * g : 64 * (g + 1), :].rearrange("p (t j) -> p t j", j=PAIRS)[:, 2 * e : 2 * e + 2, j0 : j0 + width],
+                    sums[:, PAIRS * c + j0 : PAIRS * c + j0 + width],
+                )
+
         z_bf, z_codes, z_sc = {}, {}, {}
 
         def root(b, j0, width):
             z_bf[(b, j0)] = new_tile([P, width, PACK], BF16, "zbf%d_%d" % (b, j0))
             nc.scalar.activation(
                 z_bf[(b, j0)][:].rearrange("p (g i) t -> p g t i", i=4),
-                sums[:].rearrange("p (c j) -> p c j", j=PAIRS)[:, PACK * b : PACK * (b + 1), j0 : j0 + width].rearrange("p t (g i) -> p g t i", i=4),
+                (dealt[:] if b == 0 else sums[:, PACK * PAIRS :]).rearrange("p (c j) -> p c j", j=PAIRS)[:, :, j0 : j0 + width].rearrange("p t (g i) -> p g t i", i=4),
                 ACT.Sqrt,
             )
 
-        z_rows = keep.tile([P, PACK, WIDE], BF16, name="z_rows", align_bytes=64)
+        z_rows = new_tile([P, PACK, WIDE], BF16, "z_rows")
 
         def root_row(c, j0=WIDE, j1=PAIRS):
             nc.scalar.activation(z_rows[:, c - PACK, j0 - WIDE : j1 - WIDE], sums[:, PAIRS * c + j0 : PAIRS * c + j1], ACT.Sqrt)
@@ -219,15 +251,37 @@ def tile_list_seismic_arrival_score_kernel(tc, tab_words, tab_scales, offs, pos1
                 for a in range(PASSES):
                     energy_pass(c, a, half)
 
-        gather_tab(0)
-        round_w1(0, 0, 0, nc.scalar.copy)
-        round_w1(0, 0, 1, nc.vector.tensor_copy, 0, P // 2)
-        round_w1(0, 0, 1, nc.scalar.copy, P // 2, P)
-        for u in range(2):
-            quantise_w1(0, 0, u)
-        load_w1(1, 0)
+        gather_tab(0, 0, S)
+        block = 2 * K_PASS
+        joint = keep.tile([P, 2 * block], BF16, name="joint", align_bytes=64)
+        for key, start in (((0, 0, 1), 0), ((1, 0, 0), 3 * block // 4)):
+            w_bf[key] = joint[:, start : start + block].rearrange("p (e m kk) -> p e m kk", e=2, kk=PACK)
+        w_bf[(0, 0, 0)] = new_tile([P, 2, P, PACK], BF16, "wbf0_0_0")[:]
+        round_narrow(0, 0, nc.scalar.copy)
+        quantise_w1(0, 0, 0)
+        load_narrow(1, 0)
+        load_narrow(0, 1)
+        load_narrow(1, 1)
         load_w1(0, 1)
         load_w1(1, 1)
+        for c in range(2):
+            for half in range(HALVES):
+                energy_pass(c, 0, half)
+        gather_tab(1, 0, CUT)
+        round_narrow(1, 0, lambda dst, src: nc.scalar.activation(dst, src, ACT.Identity, bias=lead[:]), 0, P // 2, 0)
+        round_narrow(1, 0, nc.scalar.copy, 0, P // 2, 1)
+        quantise_w1(1, 0, 0, 0, 1)
+        gather_tab(1, CUT, S)
+        quantise_w1(1, 0, 0, 1, 2)
+        for c in range(2):
+            for half in range(HALVES):
+                energy_pass(c, 1, half)
+        round_narrow(0, 1, nc.scalar.copy, 0, P // 8)
+        round_narrow(0, 1, nc.vector.tensor_copy, P // 8, P // 2)
+        quantise_w1(0, 0, 1)
+        for c in range(2, PACK):
+            for half in range(HALVES):
+                energy_pass(c, 0, half)
         w2_sb = new_tile([P, PASSES, 2 * N], U8, "w2_sb")
         w2_sc = new_tile([P, PASSES, N // 4], I32, "w2_sc")
         bias = new_tile([P, CLASS_TILES], F32, "bias")
@@ -240,35 +294,47 @@ def tile_list_seismic_arrival_score_kernel(tc, tab_words, tab_scales, offs, pos1
             )
         with nc.allow_non_contiguous_dma(reason="one bias value a partition"):
             nc.sync.dma_start(bias[:], b2.rearrange("(t p) -> p t", p=P))
-        for c in range(PACK):
-            for half in range(HALVES):
-                energy_pass(c, 0, half)
-        gather_tab(1)
-        round_w1(1, 0, 0, nc.scalar.copy, 0, 44)
-        round_w1(1, 0, 0, nc.vector.tensor_copy, 44, P)
-        quantise_w1(1, 0, 0, 0, 1)
-        quantise_w1(1, 0, 0, 1, 2)
-        round_w1(1, 0, 1, nc.vector.tensor_copy)
-        quantise_w1(1, 0, 1)
-        for c in range(PACK):
-            for half in range(HALVES):
-                energy_pass(c, 1, half)
 
         square(0)
         pick_first(0, 0, PAIRS)
         for c in range(1, TILES - 1):
             square(c)
-            pick_first(c, 0, PAIRS)
-            pick_add(c - 1, 0, PAIRS, 0)
+            if c == 2:
+                for j0 in (0, WIDE):
+                    pick_first(c, j0, WIDE)
+                for j0 in (0, WIDE):
+                    pick_add(c, j0, WIDE, j0)
+                deal(c)
+            else:
+                pick_first(c, 0, PAIRS)
+            if c == 1:
+                w_bf[(1, 0, 1)] = new_tile([P, 2, P, PACK], BF16, "wbf1_0_1")[:]
+                round_narrow(1, 1, lambda dst, src: nc.scalar.activation(dst, src, ACT.Identity, bias=sums[:, 0:1]), 0, P // 2, 0)
+                round_narrow(1, 1, nc.scalar.copy, 0, P // 2, 1)
+                quantise_w1(1, 0, 1, 0, 1)
+            if c == 1 or c == TILES - 2:
+                pick_add(c - 1, 0, PAIRS, 0)
+            if c == 1:
+                quantise_w1(1, 0, 1, 1, 2)
+                for late in range(2, PACK):
+                    for half in range(HALVES):
+                        energy_pass(late, 1, half)
+                deal(0)
             if c <= PACK:
                 u, a = divmod(c - 1, 2)
-                round_w1(a, 1, u, nc.scalar.copy)
+                zero_bias = second[:] if c == 2 else sums[:, PAIRS * c : PAIRS * c + 1]
+                round_w1(a, 1, u, lambda dst, src: nc.scalar.activation(dst, src, ACT.Identity, bias=zero_bias, scale=h[c + 1][:, S - 1 :]))
                 quantise_w1(a, 1, u)
+                if c != 2:
+                    pick_add(c, 0, PAIRS, 0)
+                if c in (1, 3):
+                    deal(c)
                 if a == 1:
                     energy(PACK + 2 * u)
                     energy(PACK + 2 * u + 1)
         square(TILES - 1)
-        root(0, 0, PAIRS)
+        for side in range(2):
+            root(0, WIDE * side, WIDE)
         for c in range(PACK, TILES - 2):
             root_row(c)
         for side in range(2):
@@ -284,7 +350,7 @@ def tile_list_seismic_arrival_score_kernel(tc, tab_words, tab_scales, offs, pos1
         root_row(TILES - 1, PAIRS - LAST, PAIRS)
         quantise_z(0, 0, WIDE, 0)
         quantise_z(1, 0, WIDE, 0)
-        quantise_z(0, WIDE, WIDE, 0)
+        quantise_z(0, WIDE, WIDE, WIDE)
         weave()
         quantise_z(1, WIDE, WIDE, WIDE)
         res = {}

from contextlib import ExitStack

import concourse.mybir as mybir

K, H, N, T, S, PAIRS = 1024, 1024, 512, 4096, 1024, 512
FLOPS = 2 * K * H * S + 2 * H * N * PAIRS

F32 = mybir.dt.float32
BF16 = mybir.dt.bfloat16
I32 = mybir.dt.int32
U32 = mybir.dt.uint32
U16 = mybir.dt.uint16
U8 = mybir.dt.uint8
FP8X4 = mybir.dt.float8_e4m3fn_x4
FP4X4 = mybir.dt.float4_e2m1fn_x4
ACT = mybir.ActivationFunctionType
ADD = mybir.AluOpType.add

P = 128
PACK = 4
K_PASS = P * PACK
PASSES = 2
BANK = 512
HALVES = S // BANK
TILES = H // P
CLASS_TILES = N // P
WIDE = PAIRS // 2
LAST = 64
NARROW = 256
CUT = 768


def tile_list_seismic_arrival_score_kernel(tc, tab_words, tab_scales, offs, pos1, pos2, w1, w2_words, w2_scales, b2, out):
    nc = tc.nc
    with ExitStack() as ctx:
        keep = ctx.enter_context(tc.tile_pool(name="keep", bufs=1))
        stage = ctx.enter_context(tc.tile_pool(name="stage", bufs=1))
        psum = ctx.enter_context(tc.psum_pool(name="psum", bufs=1))

        offs_sb = keep.tile([P, S // 16], U16, name="offs_sb")
        pos1_sb = keep.tile([P, PAIRS // 16], U16, name="pos1_sb")
        pos2_sb = keep.tile([P, PAIRS // 16], U16, name="pos2_sb")
        KB = 1024
        shared = {
            "tab0": 12 * KB, "raw0_1": 4 * KB + 64, "dealt": 48 * KB, "z_rows": 48 * KB, "zbf1_0": 50 * KB,
            "lead": 42 * KB, "v1_768": 42 * KB, "one": 40 * KB, "wbf1_0_1": 40 * KB, "second": 38 * KB, "wbf0_1_1": 38 * KB, "wbf1_1_1": 38 * KB, "narrow1_0": 12 * KB + 64, "narrow0_1": 16 * KB + 64, "narrow1_1": 20 * KB + 64,
            "w2_sc": 26 * KB + 64, "raw1_1": 27 * KB + 64, "w2_sb": 12 * KB + 64, "bias": 14 * KB + 64,
            "first6_0": 36 * KB, "zs0_0": 36 * KB, "zs1_0": 36 * KB + 256, "zs0_1": 36 * KB + 512,
            "wc1_1_1": 46 * KB - 512, "zbf0_0": 44 * KB, "zbf0_256": 46 * KB,
        }

        def new_tile(shape, dtype, name):
            if name in shared:
                return stage.tile(shape, dtype, name=name, offset=shared[name], align_bytes=64)
            return keep.tile(shape, dtype, name=name, align_bytes=64)

        tab_sb = [new_tile([P, T], I32, "tab%d" % a) for a in range(PASSES)]
        tab_sc = keep.tile([P, T // 4], I32, name="tab_sc", align_bytes=64)
        zero = keep.tile([P, TILES], F32, name="zero")
        sums = keep.tile([P, TILES * PAIRS], F32, name="sums", align_bytes=64)

        nc.vector.memset(tab_sc[:, : T // 8], 0)
        nc.gpsimd.memset(tab_sc[:, T // 8 :], 0)
        nc.vector.memset(zero[:], 0.0)
        h = [keep.tile([P, S], F32, name="h%d" % c, align_bytes=64) for c in range(TILES)]
        for c in range(2, 2 + PACK):
            nc.vector.memset(h[c][:, S - 1 :], 1.0)
        nc.vector.memset(h[3][:, 0:1], 1.0)
        one = new_tile([P, 1], F32, "one")
        nc.vector.memset(one[:], 1.0)
        lead = new_tile([P, 1], F32, "lead")
        nc.vector.memset(lead[:], 0.0)
        second = new_tile([P, 1], F32, "second")
        nc.vector.memset(second[:], 0.0)
        nc.scalar.activation(sums[:, 0 : TILES * PAIRS : PAIRS], zero[:], ACT.Sqrt)

        raw = {}

        def load_w1(a, b):
            raw[(a, b)] = new_tile([P, PACK, K_PASS], F32, "raw%d_%d" % (a, b))
            rows = w1[a * K_PASS : (a + 1) * K_PASS, b * K_PASS : (b + 1) * K_PASS]
            nc.sync.dma_start(raw[(a, b)][:], rows.rearrange("(p t) m -> p t m", t=PACK))

        narrow = {}

        def load_narrow(a, g):
            narrow[(a, g)] = new_tile([P, PACK, NARROW], F32, "narrow%d_%d" % (a, g))
            rows = w1[a * K_PASS : (a + 1) * K_PASS, g * NARROW : (g + 1) * NARROW]
            nc.sync.dma_start(narrow[(a, g)][:], rows.rearrange("(p t) m -> p t m", t=PACK))

        def load_tab(a, t0, t1):
            nc.sync.dma_start(tab_sb[a][:, t0:t1], tab_words[a].rearrange("p t i -> p (t i)").bitcast(I32)[:, t0:t1])

        load_tab(0, 0, T // 4)
        nc.sync.dma_start(offs_sb[:], offs)
        nc.sync.dma_start(pos1_sb[:], pos1)
        nc.sync.dma_start(pos2_sb[:], pos2)
        nc.sync.dma_start(tab_sc[0:P:4, :], tab_scales.bitcast(I32).rearrange("a q t -> q a t"))
        load_tab(0, T // 4, T)
        load_tab(1, 0, T // 2)
        load_narrow(0, 0)
        load_tab(1, T // 2, T)

        picked_sc = keep.tile([P, S], U8, name="picked_sc", align_bytes=64)
        nc.vector.tensor_copy(picked_sc[:], tab_sc[:].bitcast(U8).indirect(offs_sb[:]))
        v_sc = [keep.tile([P, S // 4], I32, name="v_sc%d" % a, align_bytes=64) for a in range(PASSES)]
        for a in range(PASSES):
            nc.vector.tensor_copy(v_sc[a][:], picked_sc[:].bitcast(I32))
            for s in range(1, 4):
                queue = nc.gpsimd if a == 1 else nc.scalar
                queue.dma_start(v_sc[a][4 * a + s : P : 32, :], picked_sc[4 * a + 8 * s : P : 32, :].bitcast(I32))

        v_codes = {}

        def gather_tab(a, i0, i1):
            v_codes[(a, i0)] = new_tile([P, i1 - i0], U32, "v%d_%d" % (a, i0))
            nc.vector.tensor_copy(v_codes[(a, i0)][:], tab_sb[a][:].bitcast(U32).indirect(offs_sb[:, i0 // 16 : i1 // 16]))

        w_bf, w_codes, w_sc = {}, {}, {}

        def round_w1(a, b, u, copy, m0=0, m1=P):
            if m0 == 0:
                w_bf[(a, b, u)] = new_tile([P, 2, P, PACK], BF16, "wbf%d_%d_%d" % (a, b, u))[:]
            copy(
                w_bf[(a, b, u)].rearrange("p e m kk -> p m kk e")[:, m0:m1, :, :],
                raw[(a, b)][:].rearrange("p kk (m t) -> p m kk t", t=PACK)[:, m0:m1, :, 2 * u : 2 * u + 2],
            )

        def round_narrow(a, g, copy, m0=0, m1=P // 2, places=slice(0, 2)):
            copy(
                w_bf[(a, 0, g)].rearrange("p e (m s) kk -> p m kk e s", s=2)[:, m0:m1, :, places],
                narrow[(a, g)][:].rearrange("p kk (m e s) -> p m kk e s", e=2, s=2)[:, m0:m1, :, places],
            )

        def quantise_w1(a, b, u, e0=0, e1=2):
            if e0 == 0:
                w_codes[(a, b, u)] = new_tile([P, 2 * P], U32, "wc%d_%d_%d" % (a, b, u))
                w_sc[(a, b, u)] = keep.tile([P, 2 * P], U8, name="ws%d_%d_%d" % (a, b, u), align_bytes=64)
            nc.vector.quantize_mx(
                out=w_codes[(a, b, u)][:, P * e0 : P * e1].bitcast(FP8X4),
                scales=w_sc[(a, b, u)][:, P * e0 : P * e1],
                in_=w_bf[(a, b, u)][:, e0:e1].rearrange("p e m kk -> p (e m kk)"),
            )

        acc = {}

        def energy_pass(c, a, half):
            b, t = divmod(c, PACK)
            u, e = divmod(t, 2)
            opens = a == 0
            if opens:
                acc[(c, half)] = psum.tile([P, BANK], F32, name="acc", tag="bank%d" % (2 * t + half))
            width = BANK // 2 if (a, half) == (1, 1) else BANK
            for i0 in range(BANK * half, BANK * (half + 1), width):
                piece = CUT if a == 1 and i0 >= CUT else 0
                nc.tensor.matmul_mx(
                    out=acc[(c, half)][:, i0 - BANK * half : i0 - BANK * half + width],
                    lhsT=w_codes[(a, b, u)][:, P * e : P * (e + 1)].bitcast(FP8X4),
                    lhsT_scale=w_sc[(a, b, u)][:, P * e : P * (e + 1)],
                    rhs=v_codes[(a, piece)][:, i0 - piece : i0 - piece + width].bitcast(FP8X4),
                    rhs_scale=v_sc[a][:].bitcast(U8)[4 * a : P, i0 : i0 + width],
                    start=opens,
                    stop=not opens and i0 + width == BANK * (half + 1),
                )

        def square(c):
            slot = PAIRS * (TILES - 1 if c <= PACK + 1 else c - 1)
            for half in range(HALVES):
                scale = {(1, 0): one[:], (2, 1): h[3][:, 0:1]}.get((c, half), 1.0)
                nc.scalar.activation(h[c][:, BANK * half : BANK * (half + 1)], acc[(c, half)][:], ACT.Square, bias=sums[:, slot : slot + 1], scale=scale)

        first = {}

        def pick_first(c, j0, width):
            if (c, j0) == (TILES - 1, 0):
                first[(c, j0)] = sums[:, PAIRS * c - width : PAIRS * c]
            else:
                first[(c, j0)] = new_tile([P, width], F32, "first%d_%d" % (c, j0))[:]
            nc.vector.tensor_copy(first[(c, j0)], h[c][:].indirect(pos1_sb[:, j0 // 16 : (j0 + width) // 16]))

        def pick_add(c, j0, width, f0):
            nc.vector.tensor_tensor(
                sums[:, PAIRS * c + j0 : PAIRS * c + j0 + width],
                h[c][:].indirect(pos2_sb[:, j0 // 16 : (j0 + width) // 16]),
                first[(c, f0)][:, j0 - f0 : j0 - f0 + width],
                ADD,
            )

        dealt = new_tile([P, PACK * PAIRS], F32, "dealt")

        def deal(c):
            g, e = divmod(c, 2)
            width = WIDE if c == PACK - 1 else PAIRS
            for j0 in range(0, PAIRS, width):
                nc.sync.dma_start(
                    dealt[64 * g : 64 * (g + 1), :].rearrange("p (t j) -> p t j", j=PAIRS)[:, 2 * e : 2 * e + 2, j0 : j0 + width],
                    sums[:, PAIRS * c + j0 : PAIRS * c + j0 + width],
                )

        z_bf, z_codes, z_sc = {}, {}, {}

        def root(b, j0, width):
            z_bf[(b, j0)] = new_tile([P, width, PACK], BF16, "zbf%d_%d" % (b, j0))
            nc.scalar.activation(
                z_bf[(b, j0)][:].rearrange("p (g i) t -> p g t i", i=4),
                (dealt[:] if b == 0 else sums[:, PACK * PAIRS :]).rearrange("p (c j) -> p c j", j=PAIRS)[:, :, j0 : j0 + width].rearrange("p t (g i) -> p g t i", i=4),
                ACT.Sqrt,
            )

        z_rows = new_tile([P, PACK, WIDE], BF16, "z_rows")

        def root_row(c, j0=WIDE, j1=PAIRS):
            nc.scalar.activation(z_rows[:, c - PACK, j0 - WIDE : j1 - WIDE], sums[:, PAIRS * c + j0 : PAIRS * c + j1], ACT.Sqrt)

        def weave():
            z_bf[(1, WIDE)] = new_tile([P, WIDE, PACK], BF16, "zbf1_%d" % WIDE)
            nc.vector.tensor_copy(
                z_bf[(1, WIDE)][:].rearrange("p (g i) t -> p g t i", i=4),
                z_rows[:].rearrange("p t (g i) -> p g t i", i=4),
            )

        def quantise_z(b, j0, width, r0):
            side, j = divmod(j0, WIDE)
            if j == 0:
                z_codes[(b, side)] = new_tile([P, WIDE], U32, "zc%d_%d" % (b, side))
                z_sc[(b, side)] = new_tile([P, WIDE], U8, "zs%d_%d" % (b, side))
            nc.vector.quantize_mx(
                out=z_codes[(b, side)][:, j : j + width].bitcast(FP8X4),
                scales=z_sc[(b, side)][:, j : j + width],
                in_=z_bf[(b, r0)][:, j0 - r0 : j0 - r0 + width, :].rearrange("p n t -> p (n t)"),
            )

        scores = {}

        def score_pass(n, side, b):
            opens = b == side
            if opens:
                scores[(n, side)] = psum.tile([P, BANK], F32, name="score", tag="bank%d" % (CLASS_TILES * side + n))
            nc.tensor.matmul_mx(
                out=scores[(n, side)][:, :WIDE],
                lhsT=w2_sb[:, b, 2 * P * n : 2 * P * (n + 1)].bitcast(FP4X4),
                lhsT_scale=w2_sc[:, b, :].bitcast(U8)[:, P * n : P * (n + 1)],
                rhs=z_codes[(b, side)][:].bitcast(FP8X4),
                rhs_scale=z_sc[(b, side)][:],
                start=opens,
                stop=not opens,
            )

        def energy(c):
            for half in range(HALVES):
                for a in range(PASSES):
                    energy_pass(c, a, half)

        gather_tab(0, 0, S)
        block = 2 * K_PASS
        joint = keep.tile([P, 2 * block], BF16, name="joint", align_bytes=64)
        for key, start in (((0, 0, 1), 0), ((1, 0, 0), 3 * block // 4)):
            w_bf[key] = joint[:, start : start + block].rearrange("p (e m kk) -> p e m kk", e=2, kk=PACK)
        w_bf[(0, 0, 0)] = new_tile([P, 2, P, PACK], BF16, "wbf0_0_0")[:]
        round_narrow(0, 0, nc.scalar.copy)
        quantise_w1(0, 0, 0)
        load_narrow(1, 0)
        load_narrow(0, 1)
        load_narrow(1, 1)
        load_w1(0, 1)
        load_w1(1, 1)
        for c in range(2):
            for half in range(HALVES):
                energy_pass(c, 0, half)
        gather_tab(1, 0, CUT)
        round_narrow(1, 0, lambda dst, src: nc.scalar.activation(dst, src, ACT.Identity, bias=lead[:]), 0, P // 2, 0)
        round_narrow(1, 0, nc.scalar.copy, 0, P // 2, 1)
        quantise_w1(1, 0, 0, 0, 1)
        gather_tab(1, CUT, S)
        quantise_w1(1, 0, 0, 1, 2)
        for c in range(2):
            for half in range(HALVES):
                energy_pass(c, 1, half)
        round_narrow(0, 1, nc.scalar.copy, 0, P // 8)
        round_narrow(0, 1, nc.vector.tensor_copy, P // 8, P // 2)
        quantise_w1(0, 0, 1)
        for c in range(2, PACK):
            for half in range(HALVES):
                energy_pass(c, 0, half)
        w2_sb = new_tile([P, PASSES, 2 * N], U8, "w2_sb")
        w2_sc = new_tile([P, PASSES, N // 4], I32, "w2_sc")
        bias = new_tile([P, CLASS_TILES], F32, "bias")
        nc.vector.memset(w2_sc[:], 0)
        nc.sync.dma_start(w2_sb[:], w2_words.rearrange("a p n -> p a n"))
        for q in range(4):
            nc.sync.dma_start(
                w2_sc[32 * q : 32 * q + 4, :, :],
                w2_scales[:, 4 * q : 4 * q + 4, :].bitcast(I32).rearrange("a g n -> g a n"),
            )
        with nc.allow_non_contiguous_dma(reason="one bias value a partition"):
            nc.sync.dma_start(bias[:], b2.rearrange("(t p) -> p t", p=P))

        square(0)
        pick_first(0, 0, PAIRS)
        for c in range(1, TILES - 1):
            square(c)
            if c == 2:
                for j0 in (0, WIDE):
                    pick_first(c, j0, WIDE)
                for j0 in (0, WIDE):
                    pick_add(c, j0, WIDE, j0)
                deal(c)
            else:
                pick_first(c, 0, PAIRS)
            if c == 1:
                w_bf[(1, 0, 1)] = new_tile([P, 2, P, PACK], BF16, "wbf1_0_1")[:]
                round_narrow(1, 1, lambda dst, src: nc.scalar.activation(dst, src, ACT.Identity, bias=sums[:, 0:1]), 0, P // 2, 0)
                round_narrow(1, 1, nc.scalar.copy, 0, P // 2, 1)
                quantise_w1(1, 0, 1, 0, 1)
            if c == 1 or c == TILES - 2:
                pick_add(c - 1, 0, PAIRS, 0)
            if c == 1:
                quantise_w1(1, 0, 1, 1, 2)
                for late in range(2, PACK):
                    for half in range(HALVES):
                        energy_pass(late, 1, half)
                deal(0)
            if c <= PACK:
                u, a = divmod(c - 1, 2)
                zero_bias = second[:] if c == 2 else sums[:, PAIRS * c : PAIRS * c + 1]
                round_w1(a, 1, u, lambda dst, src: nc.scalar.activation(dst, src, ACT.Identity, bias=zero_bias, scale=h[c + 1][:, S - 1 :]))
                quantise_w1(a, 1, u)
                if c != 2:
                    pick_add(c, 0, PAIRS, 0)
                if c in (1, 3):
                    deal(c)
                if a == 1:
                    energy(PACK + 2 * u)
                    energy(PACK + 2 * u + 1)
        square(TILES - 1)
        for side in range(2):
            root(0, WIDE * side, WIDE)
        for c in range(PACK, TILES - 2):
            root_row(c)
        for side in range(2):
            pick_first(TILES - 1, WIDE * side, WIDE)
            pick_add(TILES - 2, WIDE * side, WIDE, 0)
            if side == 0:
                pick_add(TILES - 1, 0, WIDE, 0)
        pick_add(TILES - 1, WIDE, WIDE - LAST, WIDE)
        pick_add(TILES - 1, PAIRS - LAST, LAST, WIDE)
        root(1, 0, WIDE)
        root_row(TILES - 2)
        root_row(TILES - 1, WIDE, PAIRS - LAST)
        root_row(TILES - 1, PAIRS - LAST, PAIRS)
        quantise_z(0, 0, WIDE, 0)
        quantise_z(1, 0, WIDE, 0)
        quantise_z(0, WIDE, WIDE, WIDE)
        weave()
        quantise_z(1, WIDE, WIDE, WIDE)
        res = {}
        for side in range(2):
            for n in range(CLASS_TILES):
                for b in (side, 1 - side):
                    score_pass(n, side, b)
        for side in range(2):
            for n in range(CLASS_TILES):
                res[(n, side)] = keep.tile([P, WIDE], F32, name="res%d_%d" % (n, side), align_bytes=64)
                nc.scalar.activation(res[(n, side)][:], scores[(n, side)][:, :WIDE], ACT.Sigmoid, bias=bias[:, n : n + 1])
                nc.sync.dma_start(out[P * n : P * (n + 1), WIDE * side : WIDE * (side + 1)], res[(n, side)][:])
